import numpy as np
import ml_dtypes


def mxq(x, axis, fmt="e4m3"):
    dtype, down = {"e4m3": (ml_dtypes.float8_e4m3fn, 7), "e5m2": (ml_dtypes.float8_e5m2, 14)}[fmt]
    v = np.moveaxis(np.asarray(x, np.float32).astype(ml_dtypes.bfloat16).astype(np.float64), axis, -1)
    blocks = v.reshape(v.shape[:-1] + (-1, 32))
    amax = np.abs(blocks).max(-1, keepdims=True)
    byte = np.maximum(np.where(amax > 0, np.frexp(amax)[1] - 1 + 127, 0) - down, 1)
    scale = np.exp2(byte - 127.0)
    codes = (blocks / scale).astype(np.float32).astype(dtype).astype(np.float64)
    return np.moveaxis((codes * scale).reshape(v.shape), -1, axis)


WIDE = False


def mx_kscale(k):
    if not WIDE:
        return np.ones(k)
    levels = np.array([10, -10, 5, -5, 0])
    if k % 512:
        return np.exp2(np.random.permutation(np.resize(levels, k // 32))).repeat(32)
    a = np.empty((k // 512, 16))
    for p in range(k // 512):
        a[p, :8] = np.random.permutation(np.resize(levels, 8))
        for g in range(8):
            far = levels[np.abs(levels - a[p, g]) >= 10]
            a[p, g + 8] = far[np.random.randint(len(far))]
    return np.exp2(a.ravel()).repeat(32)


def f64(x):
    return np.asarray(x).astype(np.float64)


def striped(idx):
    return np.tile(idx.reshape(-1, 16).T, (8, 1)).astype(np.uint16)


def unstriped(offs):
    return offs[:16].T.reshape(-1).astype(np.int64)


def pack_weight(w):
    k, n = w.shape
    w = f64(np.asarray(w, np.float32).astype(ml_dtypes.bfloat16)).reshape(k // 32, 32, n)
    amax = np.abs(w).max(1)
    byte = np.clip(np.where(amax > 0, np.frexp(amax)[1] - 1 + 127 - 7, 1), 1, 254)
    scaled = (w * np.exp2(127.0 - byte)[:, None, :]).reshape(k, n).astype(np.float32)
    words = np.ascontiguousarray(scaled.reshape(k // 512, 128, 4, n).transpose(0, 1, 3, 2)).astype(ml_dtypes.float8_e4m3fn).view(np.uint8)
    return words, np.ascontiguousarray(byte.astype(np.uint8).reshape(k // 512, 16, n))


def unpack_weight(words, scales):
    g, p, n, _ = words.shape
    vals = np.ascontiguousarray(words).view(ml_dtypes.float8_e4m3fn).astype(np.float64) * np.repeat(np.exp2(scales.astype(np.float64) - 127.0), 8, axis=1)[..., None]
    return vals.transpose(0, 1, 3, 2).reshape(g * 512, n)


K, T, S, D, V, H, G, R = 1024, 2048, 512, 4, 256, 512, 2048, 512
P = 2 ** 7


def setup_inputs():
    n = np.random.standard_normal
    s = mx_kscale(K)[:, None]
    u = mx_kscale(H)
    near = np.random.permutation(S)
    packed_xT = pack_weight(n((K, T)) * s)
    packed_vT = pack_weight(n((H, G)) / np.sqrt(H) / u[:, None])
    return {
        "x_words": packed_xT[0],
        "x_scales": packed_xT[1],
        "w1": (n((K, H)) / np.sqrt(K) / s * u).astype(np.float32),
        "gate": (np.tile(np.random.uniform(0.2, 1.0, (D, 1, V)) / np.sqrt(D), (1, P, 1))).astype(np.float32),
        "v_words": packed_vT[0],
        "v_scales": packed_vT[1],
        "offs": striped(np.random.permutation(T)[:S]),
        "pos1": striped(near[:V]),
        "pos2": striped(near[V:]),
        "pos3": striped(np.random.permutation(S)[:V]),
        "pos4": striped(np.random.permutation(S)[:V]),
        "cand": striped(np.random.permutation(G)[:R]),
    }


def reference(x_words, x_scales, w1, gate, v_words, v_scales, offs, pos1, pos2, pos3, pos4, cand):
    xq = unpack_weight(x_words, x_scales)[:, unstriped(offs)]
    h = mxq(f64(w1), 0, "e4m3").T @ xq
    z = h[:, unstriped(pos1)] * f64(gate)[0, :1] + h[:, unstriped(pos2)] * f64(gate)[1, :1] + h[:, unstriped(pos3)] * f64(gate)[2, :1] + h[:, unstriped(pos4)] * f64(gate)[3, :1]
    v_cand = unpack_weight(v_words, v_scales)[:, unstriped(cand)]
    y = mxq(z, 0, "e4m3").T @ v_cand
    e = np.exp(y - y.max(axis=1, keepdims=True))
    return e / e.sum(axis=1, keepdims=True)

@@ -1,0 +1,261 @@
+from contextlib import ExitStack
+
+import concourse.mybir as mybir
+from concourse.masks import make_identity
+
+K, T, S, D, V, H, G, R = 1024, 2048, 512, 4, 256, 512, 2048, 512
+FLOPS = 2 * K * H * S + 2 * H * V * R
+
+F32 = mybir.dt.float32
+BF16 = mybir.dt.bfloat16
+I32 = mybir.dt.int32
+U32 = mybir.dt.uint32
+U16 = mybir.dt.uint16
+U8 = mybir.dt.uint8
+FP8X4 = mybir.dt.float8_e4m3fn_x4
+ACT = mybir.ActivationFunctionType
+ALU = mybir.AluOpType
+AXIS = mybir.AxisListType
+
+P = 128
+PACK = 4
+PASSES = K // (P * PACK)
+TILES = H // P
+HALVES = V // P
+
+
+def tile_picked_zcbow_soft_p_kernel(
+    tc, x_words, x_scales, w1, gate, v_words, v_scales, offs, pos1, pos2, pos3, pos4, cand, out
+):
+    nc = tc.nc
+    with ExitStack() as ctx:
+        keep = ctx.enter_context(tc.tile_pool(name="keep", bufs=1))
+        psum_h = ctx.enter_context(tc.psum_pool(name="psum_h", bufs=2))
+        psum = ctx.enter_context(tc.psum_pool(name="psum", bufs=1))
+
+        def sb(name, shape, dtype, tag=None):
+            return keep.tile(shape, dtype, name=name, tag=tag or name, align_bytes=64)
+
+        def load_list(name, src):
+            tile = keep.tile(list(src.shape), U16, name=name)
+            nc.sync.dma_start(tile[:], src)
+            return tile
+
+        def load_words(name, src):
+            tile = sb(name, [P, T], U32)
+            nc.sync.dma_start(tile[:].bitcast(I32), src.rearrange("p n t -> p (n t)").bitcast(I32))
+            return tile
+
+        def load_w(name, o, c0, c1):
+            tile = sb(name, [P, PACK, c1 - c0], F32)
+            rows = w1[o * P * PACK : (o + 1) * P * PACK, c0:c1]
+            nc.sync.dma_start(tile[:], rows.rearrange("(p j) c -> p j c", j=PACK))
+            return tile
+
+        def load_scales(name, src, queue):
+            passes = src.shape[0]
+            tile = sb(name, [P, T], U8)
+            nc.vector.memset(tile[:].bitcast(I32), 0)
+            for q in range(4):
+                queue.dma_start(
+                    tile[32 * q : 32 * q + 4 * passes, :].bitcast(I32),
+                    src[:, 4 * q : 4 * q + 4, :].bitcast(I32),
+                )
+            return tile
+
+        def gather(name, table, offsets, dtype, tag=None):
+            tile = sb(name, [P, offsets.shape[1] * 16], dtype, tag)
+            nc.vector.tensor_copy(tile[:], table[:].indirect(offsets))
+            return tile
+
+        ident = sb("ident", [P, P], F32)
+        make_identity(nc, ident[:])
+        x_scale_table = load_scales("x_scale_table", x_scales, nc.gpsimd)
+        gate_rows = sb("gate_rows", [P, V], F32)
+        nc.vector.memset(gate_rows[:], 0.0)
+        warm = sb("warm", [P, 1], F32)
+        nc.scalar.dma_start(gate_rows[0:D, :], gate[:, 0, :])
+        nc.scalar.activation(warm[:], gate_rows[:, 0:1], ACT.Exp)
+        offs_t = load_list("offs_t", offs)
+        x_table = [load_words("x_table0", x_words[0])]
+        w_raw = {}
+        for o in range(PASSES):
+            w_raw[0, o] = load_w(f"w_raw0_{o}", o, 0, P)
+        x_table.append(load_words("x_table1", x_words[1]))
+        pos_t = []
+        for a in range(1, TILES):
+            for o in range(PASSES):
+                if len(pos_t) < D:
+                    pos_t.append(load_list(f"pos_t{len(pos_t)}", (pos1, pos2, pos3, pos4)[len(pos_t)]))
+                w_raw[a, o] = load_w(f"w_raw{a}_{o}", o, a * P, (a + 1) * P)
+        cand_t = load_list("cand_t", cand)
+        v_table = load_words("v_table", v_words[0])
+        v_scale_table = load_scales("v_scale_table", v_scales, nc.sync)
+
+        gate_turned = psum.tile([P, HALVES, P], F32, name="gate_turned", tag="y0")
+        for b in range(HALVES):
+            nc.tensor.transpose(gate_turned[:, b, :], gate_rows[:, b * P : (b + 1) * P], ident[:])
+        gate_cols = sb("gate_cols", [P, HALVES, D], F32)
+        nc.scalar.copy(gate_cols[:], gate_turned[:, :, 0:D])
+        gate_t = []
+        for pair in range(D // 2):
+            spread = psum.tile([P, 2, V], F32, name=f"gate_spread{pair}", tag=f"zt{pair}")
+            for e in range(2):
+                for b in range(HALVES):
+                    d = 2 * pair + e
+                    nc.tensor.transpose(
+                        spread[:, e, b * P : (b + 1) * P], gate_cols[:, b, d : d + 1].to_broadcast([P, P]), ident[:]
+                    )
+            both = sb(f"gate_pair{pair}", [P, 2, V], F32)
+            nc.scalar.copy(both[:], spread[:])
+            gate_t.extend([both[:, 0, :], both[:, 1, :]])
+
+        w_bf, w_codes, w_scale = {}, {}, {}
+
+        def cast_w(a, o, copy, tag=None):
+            w_bf[a, o] = sb(f"w_bf{a}_{o}", [P, P, PACK], BF16, tag)
+            copy(
+                w_bf[a, o][:].rearrange("p (c i) j -> p c j i", i=4),
+                w_raw[a, o][:].rearrange("p j (c i) -> p c j i", i=4),
+            )
+
+        def quantize_w(a, o, tag=None):
+            w_codes[a, o] = sb(f"w_codes{a}_{o}", [P, P], U32, tag)
+            w_scale[a, o] = sb(f"w_scale{a}_{o}", [P, P], U8)
+            nc.vector.quantize_mx(
+                out=w_codes[a, o][:].bitcast(FP8X4),
+                scales=w_scale[a, o][:],
+                in_=w_bf[a, o][:].rearrange("p c j -> p (c j)"),
+            )
+
+        h = [sb(f"h{a}", [P, S], F32) for a in range(TILES)]
+        acc = {}
+
+        def project(a, o, c0, c1):
+            if o == 0:
+                acc[a, c0] = psum_h.tile([P, c1 - c0], F32, name="h_acc")
+            nc.tensor.matmul_mx(
+                out=acc[a, c0][:],
+                lhsT=w_codes[a, o][:].bitcast(FP8X4),
+                lhsT_scale=w_scale[a, o][:],
+                rhs=x_codes[o][:, c0:c1].bitcast(FP8X4),
+                rhs_scale=x_scale[4 * o : P, c0:c1],
+                start=(o == 0),
+                stop=(o == PASSES - 1),
+            )
+
+        x_codes = [gather("x_codes0", x_table[0], offs_t[:], U32)]
+        for o in range(PASSES):
+            cast_w(0, o, nc.vector.tensor_copy)
+        for o in range(PASSES):
+            quantize_w(0, o)
+        x_scale = gather("x_scale", x_scale_table, offs_t[:], U8)
+        x_codes.append(sb("x_codes1", [P, S], U32, "x_scale_table"))
+        for c0 in (0, S // 2):
+            project(0, 0, c0, c0 + S // 2)
+        for c0 in (0, S // 2):
+            c1 = c0 + S // 2
+            nc.vector.tensor_copy(x_codes[1][:, c0:c1], x_table[1][:].indirect(offs_t[:, c0 // 16 : c1 // 16]))
+            project(0, 1, c0, c1)
+        for c0 in (0, S // 2):
+            nc.vector.tensor_copy(h[0][:, c0 : c0 + S // 2], acc[0, c0][:])
+
+        zt = [psum.tile([P, H], F32, name=f"zt{b}") for b in range(HALVES)]
+        z_bf = [sb(f"z_bf{b}", [P, 2, P, 2], BF16) for b in range(HALVES)]
+
+        def window_term(a, d, tag=None):
+            term = sb(f"term{a}_{d}", [P, V], F32, tag)
+            nc.vector.tensor_tensor(term[:], h[a][:].indirect(pos_t[d][:]), gate_t[d], ALU.mult)
+            for b in range(HALVES):
+                nc.tensor.matmul(
+                    zt[b][:, a * P : (a + 1) * P],
+                    term[:, b * P : (b + 1) * P],
+                    ident[:],
+                    start=(d == 0),
+                    stop=(d == D - 1),
+                    is_transpose=True,
+                )
+
+        def finish_h(a):
+            project(a, 1, 0, S)
+            nc.scalar.copy(h[a][:], acc[a, 0][:])
+
+        def round_z(b, a0, a1):
+            nc.scalar.copy(
+                z_bf[b][:, :, 32 * a0 : 32 * a1, :],
+                zt[b][:, a0 * P : a1 * P].rearrange("t (p u e) -> t u p e", u=2, e=2),
+            )
+
+        def score(b):
+            words = z_bf[b][:].rearrange("t u p e -> t (u p e)").bitcast(F32)
+            turned = psum.tile([P, 2, P], F32, name=f"turned{b}")
+            for u in range(2):
+                nc.tensor.transpose(turned[:, u, :], words[:, u * P : (u + 1) * P], ident[:])
+            z_in = sb(f"z_in{b}", [P, P * PACK], BF16)
+            nc.scalar.copy(
+                z_in[:].bitcast(F32).rearrange("p (t u) -> p t u", u=2), turned[:].rearrange("p u t -> p t u")
+            )
+            z_codes = sb(f"z_codes{b}", [P, P], U32)
+            z_scale = sb(f"z_scale{b}", [P, P], U8)
+            nc.vector.quantize_mx(out=z_codes[:].bitcast(FP8X4), scales=z_scale[:], in_=z_in[:])
+            y = psum.tile([P, R], F32, name=f"y{b}")
+            nc.tensor.matmul_mx(
+                out=y[:],
+                lhsT=z_codes[:].bitcast(FP8X4),
+                lhsT_scale=z_scale[:],
+                rhs=v_codes[:].bitcast(FP8X4),
+                rhs_scale=v_scale[:],
+                start=True,
+                stop=True,
+            )
+            return y
+
+        def softmax(b, y):
+            stats = sb(f"stats{b}", [P, 4], F32)
+            neg_max = sb(f"neg_max{b}", [P, 1], F32)
+            nc.vector.tensor_reduce(neg_max[:], y[:], AXIS.X, ALU.max, negate=True)
+            e = sb(f"e{b}", [P, R], F32)
+            nc.scalar.activation(e[:], y[:], ACT.Exp, bias=neg_max[:], accum_out=stats[:, 0:1])
+            nc.vector.reciprocal(stats[:, 1:2], stats[:, 0:1])
+            res = sb(f"res{b}", [P, R], F32)
+            nc.vector.tensor_scalar(res[:], e[:], stats[:, 1:2], None, ALU.mult)
+            nc.sync.dma_start(out[b * P : (b + 1) * P, :], res[:])
+
+        for a in (1, 2):
+            for o in range(PASSES):
+                cast_w(a, o, nc.scalar.copy)
+        quantize_w(1, 0, "x_table1")
+        project(1, 0, 0, S)
+        window_term(0, 0)
+        window_term(0, 1)
+        quantize_w(1, 1, "term0_0")
+        finish_h(1)
+        window_term(0, 2, "w_bf1_1")
+        window_term(0, 3)
+        quantize_w(2, 0, "w_bf1_1")
+        quantize_w(2, 1, "term0_1")
+        project(2, 0, 0, S)
+        finish_h(2)
+        cast_w(3, 0, nc.scalar.copy, "term0_0")
+        cast_w(3, 1, nc.scalar.copy, "x_table1")
+        window_term(1, 0, "w_bf2_1")
+        window_term(1, 1)
+        window_term(1, 2)
+        quantize_w(3, 0, "term1_1")
+        quantize_w(3, 1, "w_bf2_1")
+        project(3, 0, 0, S)
+        finish_h(3)
+        window_term(1, 3, "w_bf3_1")
+        for d in range(D):
+            window_term(2, d)
+        for b in range(HALVES):
+            round_z(b, 0, 3)
+        for d in range(D):
+            window_term(3, d)
+        v_scale = gather("v_scale", v_scale_table, cand_t[:], U8, "h3")
+        v_codes = gather("v_codes", v_table, cand_t[:], U32, "gate_pair1")
+        for b in range(HALVES):
+            round_z(b, 3, 4)
+        y = [score(b) for b in range(HALVES)]
+        for b in range(HALVES):
+            softmax(b, y[b])

@@ -52,11 +52,11 @@ def tile_picked_zcbow_soft_p_kernel(
             nc.sync.dma_start(tile[:], rows.rearrange("(p j) c -> p j c", j=PACK))
             return tile
 
-        def load_scales(name, src, queue):
+        def load_scales(name, src, clear, queues):
             passes = src.shape[0]
             tile = sb(name, [P, T], U8)
-            nc.vector.memset(tile[:].bitcast(I32), 0)
-            for q in range(4):
+            clear.memset(tile[:].bitcast(I32), 0)
+            for q, queue in enumerate(queues):
                 queue.dma_start(
                     tile[32 * q : 32 * q + 4 * passes, :].bitcast(I32),
                     src[:, 4 * q : 4 * q + 4, :].bitcast(I32),
@@ -70,13 +70,13 @@ def tile_picked_zcbow_soft_p_kernel(
 
         ident = sb("ident", [P, P], F32)
         make_identity(nc, ident[:])
-        x_scale_table = load_scales("x_scale_table", x_scales, nc.gpsimd)
-        gate_rows = sb("gate_rows", [P, V], F32)
-        nc.vector.memset(gate_rows[:], 0.0)
-        warm = sb("warm", [P, 1], F32)
-        nc.scalar.dma_start(gate_rows[0:D, :], gate[:, 0, :])
-        nc.scalar.activation(warm[:], gate_rows[:, 0:1], ACT.Exp)
+        x_scale_table = load_scales("x_scale_table", x_scales, nc.vector, (nc.gpsimd,) * 4)
+        warm = sb("warm", [P, 2], F32)
+        nc.vector.memset(warm[:], 0.0)
+        nc.scalar.activation(warm[:, 1:2], warm[:, 0:1], ACT.Exp)
         offs_t = load_list("offs_t", offs)
+        gate_rows = sb("gate_rows", [P, P], F32)
+        nc.sync.dma_start(gate_rows[:], gate.rearrange("d p (b t) -> (d p b) t", t=P)[0 : 7 * P : 7, :])
         x_table = [load_words("x_table0", x_words[0])]
         w_raw = {}
         for o in range(PASSES):
@@ -90,21 +90,21 @@ def tile_picked_zcbow_soft_p_kernel(
                 w_raw[a, o] = load_w(f"w_raw{a}_{o}", o, a * P, (a + 1) * P)
         cand_t = load_list("cand_t", cand)
         v_table = load_words("v_table", v_words[0])
-        v_scale_table = load_scales("v_scale_table", v_scales, nc.sync)
+        v_scale_table = load_scales("v_scale_table", v_scales, nc.vector, (nc.sync,) * 4)
 
-        gate_turned = psum.tile([P, HALVES, P], F32, name="gate_turned", tag="y0")
-        for b in range(HALVES):
-            nc.tensor.transpose(gate_turned[:, b, :], gate_rows[:, b * P : (b + 1) * P], ident[:])
-        gate_cols = sb("gate_cols", [P, HALVES, D], F32)
-        nc.scalar.copy(gate_cols[:], gate_turned[:, :, 0:D])
+        gate_turned = psum.tile([P, P], F32, name="gate_turned", tag="y0")
+        nc.tensor.transpose(gate_turned[:], gate_rows[:], ident[:])
+        gate_cols = sb("gate_cols", [P, P], F32)
+        nc.scalar.copy(gate_cols[:], gate_turned[:])
         gate_t = []
         for pair in range(D // 2):
             spread = psum.tile([P, 2, V], F32, name=f"gate_spread{pair}", tag=f"zt{pair}")
             for e in range(2):
                 for b in range(HALVES):
                     d = 2 * pair + e
+                    col = min(q for q in range(P) if 7 * q // V == d and q % 2 == b)
                     nc.tensor.transpose(
-                        spread[:, e, b * P : (b + 1) * P], gate_cols[:, b, d : d + 1].to_broadcast([P, P]), ident[:]
+                        spread[:, e, b * P : (b + 1) * P], gate_cols[:, col : col + 1].to_broadcast([P, P]), ident[:]
                     )
             both = sb(f"gate_pair{pair}", [P, 2, V], F32)
             nc.scalar.copy(both[:], spread[:])
@@ -163,13 +163,16 @@ def tile_picked_zcbow_soft_p_kernel(
         zt = [psum.tile([P, H], F32, name=f"zt{b}") for b in range(HALVES)]
         z_bf = [sb(f"z_bf{b}", [P, 2, P, 2], BF16) for b in range(HALVES)]
 
-        def window_term(a, d, tag=None):
-            term = sb(f"term{a}_{d}", [P, V], F32, tag)
-            nc.vector.tensor_tensor(term[:], h[a][:].indirect(pos_t[d][:]), gate_t[d], ALU.mult)
-            for b in range(HALVES):
+        def window_term(a, d, tag=None, halves=(0, 1)):
+            t0, t1 = halves[0] * P, (halves[-1] + 1) * P
+            term = sb(f"term{a}_{d}_{t0}" if t0 else f"term{a}_{d}", [P, t1 - t0], F32, tag)
+            nc.vector.tensor_tensor(
+                term[:], h[a][:].indirect(pos_t[d][:, t0 // 16 : t1 // 16]), gate_t[d][:, t0:t1], ALU.mult
+            )
+            for b in halves:
                 nc.tensor.matmul(
                     zt[b][:, a * P : (a + 1) * P],
-                    term[:, b * P : (b + 1) * P],
+                    term[:, b * P - t0 : (b + 1) * P - t0],
                     ident[:],
                     start=(d == 0),
                     stop=(d == D - 1),
@@ -250,12 +253,12 @@ def tile_picked_zcbow_soft_p_kernel(
             window_term(2, d)
         for b in range(HALVES):
             round_z(b, 0, 3)
-        for d in range(D):
-            window_term(3, d)
+        for b in range(HALVES):
+            for d in range(D):
+                window_term(3, d, halves=(b,))
+            round_z(b, 3, 4)
         v_scale = gather("v_scale", v_scale_table, cand_t[:], U8, "h3")
         v_codes = gather("v_codes", v_table, cand_t[:], U32, "gate_pair1")
-        for b in range(HALVES):
-            round_z(b, 3, 4)
         y = [score(b) for b in range(HALVES)]
         for b in range(HALVES):
             softmax(b, y[b])

@@ -30,7 +30,6 @@ def tile_picked_zcbow_soft_p_kernel(
     nc = tc.nc
     with ExitStack() as ctx:
         keep = ctx.enter_context(tc.tile_pool(name="keep", bufs=1))
-        psum_h = ctx.enter_context(tc.psum_pool(name="psum_h", bufs=2))
         psum = ctx.enter_context(tc.psum_pool(name="psum", bufs=1))
 
         def sb(name, shape, dtype, tag=None):
@@ -70,35 +69,33 @@ def tile_picked_zcbow_soft_p_kernel(
 
         ident = sb("ident", [P, P], F32)
         make_identity(nc, ident[:])
-        x_scale_table = load_scales("x_scale_table", x_scales, nc.vector, (nc.gpsimd,) * 4)
-        warm = sb("warm", [P, 2], F32)
-        nc.vector.memset(warm[:], 0.0)
-        nc.scalar.activation(warm[:, 1:2], warm[:, 0:1], ACT.Exp)
         offs_t = load_list("offs_t", offs)
         gate_rows = sb("gate_rows", [P, P], F32)
         nc.sync.dma_start(gate_rows[:], gate.rearrange("d p (b t) -> (d p b) t", t=P)[0 : 7 * P : 7, :])
         x_table = [load_words("x_table0", x_words[0])]
+        x_scale_table = load_scales("x_scale_table", x_scales, nc.vector, (nc.gpsimd,) * 3 + (nc.sync,))
+        warm = sb("warm", [P, 2], F32)
+        nc.vector.memset(warm[:], 0.0)
+        nc.scalar.activation(warm[:, 1:2], warm[:, 0:1], ACT.Exp)
         w_raw = {}
         for o in range(PASSES):
-            w_raw[0, o] = load_w(f"w_raw0_{o}", o, 0, P)
+            w_raw[0, o] = load_w(f"w_raw0_{o}", o, 0, P)[:]
         x_table.append(load_words("x_table1", x_words[1]))
-        pos_t = []
+        pos_t = [load_list(f"pos_t{d}", src) for d, src in enumerate((pos1, pos2, pos3, pos4))]
+        cand_t = load_list("cand_t", cand)
         for a in range(1, TILES):
             for o in range(PASSES):
-                if len(pos_t) < D:
-                    pos_t.append(load_list(f"pos_t{len(pos_t)}", (pos1, pos2, pos3, pos4)[len(pos_t)]))
-                w_raw[a, o] = load_w(f"w_raw{a}_{o}", o, a * P, (a + 1) * P)
-        cand_t = load_list("cand_t", cand)
+                w_raw[a, o] = load_w(f"w_raw{a}_{o}", o, a * P, (a + 1) * P)[:]
         v_table = load_words("v_table", v_words[0])
-        v_scale_table = load_scales("v_scale_table", v_scales, nc.vector, (nc.sync,) * 4)
+        v_scale_table = load_scales("v_scale_table", v_scales, nc.gpsimd, (nc.sync,) * 4)
 
-        gate_turned = psum.tile([P, P], F32, name="gate_turned", tag="y0")
+        gate_turned = psum.tile([P, P], F32, name="gate_turned", tag="h_bank0")
         nc.tensor.transpose(gate_turned[:], gate_rows[:], ident[:])
         gate_cols = sb("gate_cols", [P, P], F32)
         nc.scalar.copy(gate_cols[:], gate_turned[:])
         gate_t = []
         for pair in range(D // 2):
-            spread = psum.tile([P, 2, V], F32, name=f"gate_spread{pair}", tag=f"zt{pair}")
+            spread = psum.tile([P, 2, V], F32, name=f"gate_spread{pair}", tag=f"h_bank{1 - pair}")
             for e in range(2):
                 for b in range(HALVES):
                     d = 2 * pair + e
@@ -110,34 +107,34 @@ def tile_picked_zcbow_soft_p_kernel(
             nc.scalar.copy(both[:], spread[:])
             gate_t.extend([both[:, 0, :], both[:, 1, :]])
 
-        w_bf, w_codes, w_scale = {}, {}, {}
+        w_bf, w_codes, w_scale, h = {}, {}, {}, {}
 
-        def cast_w(a, o, copy, tag=None):
-            w_bf[a, o] = sb(f"w_bf{a}_{o}", [P, P, PACK], BF16, tag)
-            copy(
-                w_bf[a, o][:].rearrange("p (c i) j -> p c j i", i=4),
-                w_raw[a, o][:].rearrange("p j (c i) -> p c j i", i=4),
-            )
+        def cast_w(a, copy, tag=None):
+            w_bf[a] = sb(f"w_bf{a}", [P, PASSES, P, PACK], BF16, tag)
+            for o in range(PASSES):
+                copy(
+                    w_bf[a][:, o, :, :].rearrange("p (c i) j -> p c j i", i=4),
+                    w_raw[a, o].rearrange("p j (c i) -> p c j i", i=4),
+                )
 
-        def quantize_w(a, o, tag=None):
-            w_codes[a, o] = sb(f"w_codes{a}_{o}", [P, P], U32, tag)
-            w_scale[a, o] = sb(f"w_scale{a}_{o}", [P, P], U8)
+        def quantize_w(a, tag=None):
+            w_codes[a] = sb(f"w_codes{a}", [P, PASSES, P], U32, tag)
+            w_scale[a] = sb(f"w_scale{a}", [P, PASSES, P], U8)
             nc.vector.quantize_mx(
-                out=w_codes[a, o][:].bitcast(FP8X4),
-                scales=w_scale[a, o][:],
-                in_=w_bf[a, o][:].rearrange("p c j -> p (c j)"),
+                out=w_codes[a][:].rearrange("p o c -> p (o c)").bitcast(FP8X4),
+                scales=w_scale[a][:].rearrange("p o c -> p (o c)"),
+                in_=w_bf[a][:].rearrange("p o c j -> p (o c j)"),
             )
 
-        h = [sb(f"h{a}", [P, S], F32) for a in range(TILES)]
         acc = {}
 
         def project(a, o, c0, c1):
             if o == 0:
-                acc[a, c0] = psum_h.tile([P, c1 - c0], F32, name="h_acc")
+                acc[a, c0] = psum.tile([P, c1 - c0], F32, name=f"h_acc{a}_{c0}", tag=f"h_bank{(len(acc) + 1) % 2}")
             nc.tensor.matmul_mx(
                 out=acc[a, c0][:],
-                lhsT=w_codes[a, o][:].bitcast(FP8X4),
-                lhsT_scale=w_scale[a, o][:],
+                lhsT=w_codes[a][:, o, :].bitcast(FP8X4),
+                lhsT_scale=w_scale[a][:, o, :],
                 rhs=x_codes[o][:, c0:c1].bitcast(FP8X4),
                 rhs_scale=x_scale[4 * o : P, c0:c1],
                 start=(o == 0),
@@ -145,11 +142,9 @@ def tile_picked_zcbow_soft_p_kernel(
             )
 
         x_codes = [gather("x_codes0", x_table[0], offs_t[:], U32)]
-        for o in range(PASSES):
-            cast_w(0, o, nc.vector.tensor_copy)
-        for o in range(PASSES):
-            quantize_w(0, o)
+        cast_w(0, nc.vector.tensor_copy)
         x_scale = gather("x_scale", x_scale_table, offs_t[:], U8)
+        quantize_w(0)
         x_codes.append(sb("x_codes1", [P, S], U32, "x_scale_table"))
         for c0 in (0, S // 2):
             project(0, 0, c0, c0 + S // 2)
@@ -157,6 +152,7 @@ def tile_picked_zcbow_soft_p_kernel(
             c1 = c0 + S // 2
             nc.vector.tensor_copy(x_codes[1][:, c0:c1], x_table[1][:].indirect(offs_t[:, c0 // 16 : c1 // 16]))
             project(0, 1, c0, c1)
+        h[0] = sb("h0", [P, S], F32)
         for c0 in (0, S // 2):
             nc.vector.tensor_copy(h[0][:, c0 : c0 + S // 2], acc[0, c0][:])
 
@@ -179,8 +175,10 @@ def tile_picked_zcbow_soft_p_kernel(
                     is_transpose=True,
                 )
 
-        def finish_h(a):
-            project(a, 1, 0, S)
+        def finish_h(a, tag=None):
+            for o in range(PASSES):
+                project(a, o, 0, S)
+            h[a] = sb(f"h{a}", [P, S], F32, tag)
             nc.scalar.copy(h[a][:], acc[a, 0][:])
 
         def round_z(b, a0, a1):
@@ -224,31 +222,23 @@ def tile_picked_zcbow_soft_p_kernel(
             nc.vector.tensor_scalar(res[:], e[:], stats[:, 1:2], None, ALU.mult)
             nc.sync.dma_start(out[b * P : (b + 1) * P, :], res[:])
 
-        for a in (1, 2):
-            for o in range(PASSES):
-                cast_w(a, o, nc.scalar.copy)
-        quantize_w(1, 0, "x_table1")
-        project(1, 0, 0, S)
-        window_term(0, 0)
+        cast_w(1, nc.scalar.copy)
+        cast_w(2, nc.scalar.copy)
+        quantize_w(1, "x_table1")
+        finish_h(1, "w_raw2_1")
+        window_term(0, 0, "w_bf1")
         window_term(0, 1)
-        quantize_w(1, 1, "term0_0")
-        finish_h(1)
-        window_term(0, 2, "w_bf1_1")
-        window_term(0, 3)
-        quantize_w(2, 0, "w_bf1_1")
-        quantize_w(2, 1, "term0_1")
-        project(2, 0, 0, S)
-        finish_h(2)
-        cast_w(3, 0, nc.scalar.copy, "term0_0")
-        cast_w(3, 1, nc.scalar.copy, "x_table1")
-        window_term(1, 0, "w_bf2_1")
+        window_term(0, 2)
+        quantize_w(2, "term0_1")
+        cast_w(3, nc.scalar.copy, "x_table1")
+        finish_h(2, "w_raw3_1")
+        window_term(0, 3, "w_bf2")
+        window_term(1, 0)
         window_term(1, 1)
-        window_term(1, 2)
-        quantize_w(3, 0, "term1_1")
-        quantize_w(3, 1, "w_bf2_1")
-        project(3, 0, 0, S)
+        quantize_w(3, "term1_0")
         finish_h(3)
-        window_term(1, 3, "w_bf3_1")
+        window_term(1, 2, "x_table1")
+        window_term(1, 3)
         for d in range(D):
             window_term(2, d)
         for b in range(HALVES):
@@ -257,8 +247,8 @@ def tile_picked_zcbow_soft_p_kernel(
             for d in range(D):
                 window_term(3, d, halves=(b,))
             round_z(b, 3, 4)
-        v_scale = gather("v_scale", v_scale_table, cand_t[:], U8, "h3")
-        v_codes = gather("v_codes", v_table, cand_t[:], U32, "gate_pair1")
+        v_scale = gather("v_scale", v_scale_table, cand_t[:], U8, "term3_2_128")
+        v_codes = gather("v_codes", v_table, cand_t[:], U32, "term3_1_128")
         y = [score(b) for b in range(HALVES)]
         for b in range(HALVES):
             softmax(b, y[b])

@@ -67,45 +67,32 @@ def tile_picked_zcbow_soft_p_kernel(
             nc.vector.tensor_copy(tile[:], table[:].indirect(offsets))
             return tile
 
-        ident = sb("ident", [P, P], F32)
-        make_identity(nc, ident[:])
         offs_t = load_list("offs_t", offs)
-        gate_rows = sb("gate_rows", [P, P], F32)
-        nc.sync.dma_start(gate_rows[:], gate.rearrange("d p (b t) -> (d p b) t", t=P)[0 : 7 * P : 7, :])
+        cand_t = load_list("cand_t", cand)
         x_table = [load_words("x_table0", x_words[0])]
-        x_scale_table = load_scales("x_scale_table", x_scales, nc.vector, (nc.gpsimd,) * 3 + (nc.sync,))
-        warm = sb("warm", [P, 2], F32)
-        nc.vector.memset(warm[:], 0.0)
-        nc.scalar.activation(warm[:, 1:2], warm[:, 0:1], ACT.Exp)
+        x_scale_table = load_scales("x_scale_table", x_scales, nc.gpsimd, (nc.gpsimd, nc.gpsimd, nc.sync, nc.sync))
         w_raw = {}
         for o in range(PASSES):
             w_raw[0, o] = load_w(f"w_raw0_{o}", o, 0, P)[:]
+        v_scale_table = load_scales("v_scale_table", v_scales, nc.vector, (nc.sync,) * 4)
+        warm = sb("warm", [P, 2], F32)
+        nc.vector.memset(warm[:], 0.0)
+        nc.scalar.activation(warm[:, 1:2], warm[:, 0:1], ACT.Exp)
+        ident = sb("ident", [P, P], F32)
+        make_identity(nc, ident[:])
         x_table.append(load_words("x_table1", x_words[1]))
-        pos_t = [load_list(f"pos_t{d}", src) for d, src in enumerate((pos1, pos2, pos3, pos4))]
-        cand_t = load_list("cand_t", cand)
-        for a in range(1, TILES):
+        for o in range(PASSES):
+            w_raw[1, o] = load_w(f"w_raw1_{o}", o, P, 2 * P)[:]
+        pos_t, gate_t = [], []
+        for pair, lists in enumerate(((pos1, pos2), (pos3, pos4))):
+            pos_t.extend(load_list(f"pos_t{2 * pair + e}", src) for e, src in enumerate(lists))
+            both = sb(f"gate_pair{pair}", [P, 2, V], F32)
+            nc.sync.dma_start(both[:], gate[2 * pair : 2 * pair + 2].rearrange("d p t -> p d t"))
+            gate_t.extend([both[:, 0, :], both[:, 1, :]])
+        for a in range(2, TILES):
             for o in range(PASSES):
                 w_raw[a, o] = load_w(f"w_raw{a}_{o}", o, a * P, (a + 1) * P)[:]
         v_table = load_words("v_table", v_words[0])
-        v_scale_table = load_scales("v_scale_table", v_scales, nc.gpsimd, (nc.sync,) * 4)
-
-        gate_turned = psum.tile([P, P], F32, name="gate_turned", tag="h_bank0")
-        nc.tensor.transpose(gate_turned[:], gate_rows[:], ident[:])
-        gate_cols = sb("gate_cols", [P, P], F32)
-        nc.scalar.copy(gate_cols[:], gate_turned[:])
-        gate_t = []
-        for pair in range(D // 2):
-            spread = psum.tile([P, 2, V], F32, name=f"gate_spread{pair}", tag=f"h_bank{1 - pair}")
-            for e in range(2):
-                for b in range(HALVES):
-                    d = 2 * pair + e
-                    col = min(q for q in range(P) if 7 * q // V == d and q % 2 == b)
-                    nc.tensor.transpose(
-                        spread[:, e, b * P : (b + 1) * P], gate_cols[:, col : col + 1].to_broadcast([P, P]), ident[:]
-                    )
-            both = sb(f"gate_pair{pair}", [P, 2, V], F32)
-            nc.scalar.copy(both[:], spread[:])
-            gate_t.extend([both[:, 0, :], both[:, 1, :]])
 
         w_bf, w_codes, w_scale, h = {}, {}, {}, {}
 
@@ -142,8 +129,9 @@ def tile_picked_zcbow_soft_p_kernel(
             )
 
         x_codes = [gather("x_codes0", x_table[0], offs_t[:], U32)]
-        cast_w(0, nc.vector.tensor_copy)
+        cast_w(0, nc.scalar.copy)
         x_scale = gather("x_scale", x_scale_table, offs_t[:], U8)
+        v_scale = gather("v_scale", v_scale_table, cand_t[:], U8)
         quantize_w(0)
         x_codes.append(sb("x_codes1", [P, S], U32, "x_scale_table"))
         for c0 in (0, S // 2):
@@ -224,22 +212,23 @@ def tile_picked_zcbow_soft_p_kernel(
 
         cast_w(1, nc.scalar.copy)
         cast_w(2, nc.scalar.copy)
-        quantize_w(1, "x_table1")
+        quantize_w(1, "w_codes0")
         finish_h(1, "w_raw2_1")
-        window_term(0, 0, "w_bf1")
-        window_term(0, 1)
-        window_term(0, 2)
-        quantize_w(2, "term0_1")
-        cast_w(3, nc.scalar.copy, "x_table1")
+        window_term(0, 0)
+        window_term(0, 1, "w_bf1")
+        quantize_w(2, "term0_0")
+        cast_w(3, nc.scalar.copy, "w_codes0")
         finish_h(2, "w_raw3_1")
-        window_term(0, 3, "w_bf2")
-        window_term(1, 0)
+        window_term(0, 2)
+        window_term(0, 3)
+        window_term(1, 0, "w_bf2")
         window_term(1, 1)
-        quantize_w(3, "term1_0")
+        quantize_w(3, "w_bf2")
         finish_h(3)
-        window_term(1, 2, "x_table1")
+        window_term(1, 2)
         window_term(1, 3)
-        for d in range(D):
+        window_term(2, 0, "w_codes0")
+        for d in range(1, D):
             window_term(2, d)
         for b in range(HALVES):
             round_z(b, 0, 3)
@@ -247,8 +236,7 @@ def tile_picked_zcbow_soft_p_kernel(
             for d in range(D):
                 window_term(3, d, halves=(b,))
             round_z(b, 3, 4)
-        v_scale = gather("v_scale", v_scale_table, cand_t[:], U8, "term3_2_128")
-        v_codes = gather("v_codes", v_table, cand_t[:], U32, "term3_1_128")
+        v_codes = gather("v_codes", v_table, cand_t[:], U32, "term3_2_128")
         y = [score(b) for b in range(HALVES)]
         for b in range(HALVES):
             softmax(b, y[b])

@@ -67,32 +67,51 @@ def tile_picked_zcbow_soft_p_kernel(
             nc.vector.tensor_copy(tile[:], table[:].indirect(offsets))
             return tile
 
+        ident = sb("ident", [P, P], F32)
+        make_identity(nc, ident[:])
         offs_t = load_list("offs_t", offs)
         cand_t = load_list("cand_t", cand)
         x_table = [load_words("x_table0", x_words[0])]
-        x_scale_table = load_scales("x_scale_table", x_scales, nc.gpsimd, (nc.gpsimd, nc.gpsimd, nc.sync, nc.sync))
-        w_raw = {}
-        for o in range(PASSES):
-            w_raw[0, o] = load_w(f"w_raw0_{o}", o, 0, P)[:]
-        v_scale_table = load_scales("v_scale_table", v_scales, nc.vector, (nc.sync,) * 4)
+        x_scale_table = load_scales("x_scale_table", x_scales, nc.vector, (nc.gpsimd, nc.gpsimd, nc.scalar, nc.scalar))
+        v_scale_table = sb("v_scale_table", [P, G], U8)
+        nc.vector.memset(v_scale_table[:].bitcast(I32), 0)
+        nc.scalar.dma_start(v_scale_table[0:P:8, :].bitcast(I32), v_scales[0].bitcast(I32))
+        gate_rows = sb("gate_rows", [P, P], F32)
+        nc.vector.memset(gate_rows[:], 0.0)
+        nc.sync.dma_start(gate_rows[0 : D * HALVES, :], gate[:, 0, :].rearrange("d (b t) -> d b t", t=P))
         warm = sb("warm", [P, 2], F32)
         nc.vector.memset(warm[:], 0.0)
         nc.scalar.activation(warm[:, 1:2], warm[:, 0:1], ACT.Exp)
-        ident = sb("ident", [P, P], F32)
-        make_identity(nc, ident[:])
+        v_scale = sb("v_scale", [P, R], U8)
+        nc.vector.memset(v_scale[:].bitcast(I32), 0)
+        w_raw = {}
+        for o in range(PASSES):
+            w_raw[0, o] = load_w(f"w_raw0_{o}", o, 0, P)[:]
         x_table.append(load_words("x_table1", x_words[1]))
         for o in range(PASSES):
             w_raw[1, o] = load_w(f"w_raw1_{o}", o, P, 2 * P)[:]
-        pos_t, gate_t = [], []
-        for pair, lists in enumerate(((pos1, pos2), (pos3, pos4))):
-            pos_t.extend(load_list(f"pos_t{2 * pair + e}", src) for e, src in enumerate(lists))
-            both = sb(f"gate_pair{pair}", [P, 2, V], F32)
-            nc.sync.dma_start(both[:], gate[2 * pair : 2 * pair + 2].rearrange("d p t -> p d t"))
-            gate_t.extend([both[:, 0, :], both[:, 1, :]])
+        pos_t = [load_list(f"pos_t{d}", src) for d, src in enumerate((pos1, pos2, pos3, pos4))]
         for a in range(2, TILES):
             for o in range(PASSES):
                 w_raw[a, o] = load_w(f"w_raw{a}_{o}", o, a * P, (a + 1) * P)[:]
         v_table = load_words("v_table", v_words[0])
+
+        gate_turned = psum.tile([P, P], F32, name="gate_turned", tag="h_bank0")
+        nc.tensor.transpose(gate_turned[:], gate_rows[:], ident[:])
+        gate_cols = sb("gate_cols", [P, D * HALVES], F32)
+        nc.scalar.copy(gate_cols[:], gate_turned[:, 0 : D * HALVES])
+        gate_t = []
+        for pair in range(D // 2):
+            spread = psum.tile([P, 2, V], F32, name=f"gate_spread{pair}", tag=f"h_bank{1 - pair}")
+            for e in range(2):
+                for b in range(HALVES):
+                    col = (2 * pair + e) * HALVES + b
+                    nc.tensor.transpose(
+                        spread[:, e, b * P : (b + 1) * P], gate_cols[:, col : col + 1].to_broadcast([P, P]), ident[:]
+                    )
+            both = sb(f"gate_pair{pair}", [P, 2, V], F32)
+            nc.scalar.copy(both[:], spread[:])
+            gate_t.extend([both[:, 0, :], both[:, 1, :]])
 
         w_bf, w_codes, w_scale, h = {}, {}, {}, {}
 
@@ -128,10 +147,12 @@ def tile_picked_zcbow_soft_p_kernel(
                 stop=(o == PASSES - 1),
             )
 
+        v_scale_spread = gather("v_scale_spread", v_scale_table, cand_t[:], U8)
+        for r in range(4):
+            nc.sync.dma_start(v_scale[r:P:32, :].bitcast(I32), v_scale_spread[8 * r : P : 32, :].bitcast(I32))
         x_codes = [gather("x_codes0", x_table[0], offs_t[:], U32)]
         cast_w(0, nc.scalar.copy)
-        x_scale = gather("x_scale", x_scale_table, offs_t[:], U8)
-        v_scale = gather("v_scale", v_scale_table, cand_t[:], U8)
+        x_scale = gather("x_scale", x_scale_table, offs_t[:], U8, "x_table0")
         quantize_w(0)
         x_codes.append(sb("x_codes1", [P, S], U32, "x_scale_table"))
         for c0 in (0, S // 2):
@@ -210,20 +231,20 @@ def tile_picked_zcbow_soft_p_kernel(
             nc.vector.tensor_scalar(res[:], e[:], stats[:, 1:2], None, ALU.mult)
             nc.sync.dma_start(out[b * P : (b + 1) * P, :], res[:])
 
-        cast_w(1, nc.scalar.copy)
-        cast_w(2, nc.scalar.copy)
+        cast_w(1, nc.scalar.copy, "gate_cols")
+        cast_w(2, nc.scalar.copy, "w_raw1_1")
         quantize_w(1, "w_codes0")
         finish_h(1, "w_raw2_1")
         window_term(0, 0)
-        window_term(0, 1, "w_bf1")
+        window_term(0, 1, "gate_cols")
         quantize_w(2, "term0_0")
         cast_w(3, nc.scalar.copy, "w_codes0")
         finish_h(2, "w_raw3_1")
         window_term(0, 2)
         window_term(0, 3)
-        window_term(1, 0, "w_bf2")
+        window_term(1, 0, "w_raw1_1")
         window_term(1, 1)
-        quantize_w(3, "w_bf2")
+        quantize_w(3, "w_raw1_1")
         finish_h(3)
         window_term(1, 2)
         window_term(1, 3)

@@ -69,16 +69,15 @@ def tile_picked_zcbow_soft_p_kernel(
 
         ident = sb("ident", [P, P], F32)
         make_identity(nc, ident[:])
+        x_table = [load_words("x_table0", x_words[0])]
         offs_t = load_list("offs_t", offs)
         cand_t = load_list("cand_t", cand)
-        x_table = [load_words("x_table0", x_words[0])]
         x_scale_table = load_scales("x_scale_table", x_scales, nc.vector, (nc.gpsimd, nc.gpsimd, nc.scalar, nc.scalar))
         v_scale_table = sb("v_scale_table", [P, G], U8)
         nc.vector.memset(v_scale_table[:].bitcast(I32), 0)
         nc.scalar.dma_start(v_scale_table[0:P:8, :].bitcast(I32), v_scales[0].bitcast(I32))
         gate_rows = sb("gate_rows", [P, P], F32)
         nc.vector.memset(gate_rows[:], 0.0)
-        nc.sync.dma_start(gate_rows[0 : D * HALVES, :], gate[:, 0, :].rearrange("d (b t) -> d b t", t=P))
         warm = sb("warm", [P, 2], F32)
         nc.vector.memset(warm[:], 0.0)
         nc.scalar.activation(warm[:, 1:2], warm[:, 0:1], ACT.Exp)
@@ -87,6 +86,7 @@ def tile_picked_zcbow_soft_p_kernel(
         w_raw = {}
         for o in range(PASSES):
             w_raw[0, o] = load_w(f"w_raw0_{o}", o, 0, P)[:]
+        nc.sync.dma_start(gate_rows[0 : D * HALVES, :], gate[:, 0, :].rearrange("d (b t) -> d b t", t=P))
         x_table.append(load_words("x_table1", x_words[1]))
         for o in range(PASSES):
             w_raw[1, o] = load_w(f"w_raw1_{o}", o, P, 2 * P)[:]
@@ -227,9 +227,18 @@ def tile_picked_zcbow_soft_p_kernel(
             e = sb(f"e{b}", [P, R], F32)
             nc.scalar.activation(e[:], y[:], ACT.Exp, bias=neg_max[:], accum_out=stats[:, 0:1])
             nc.vector.reciprocal(stats[:, 1:2], stats[:, 0:1])
-            res = sb(f"res{b}", [P, R], F32)
-            nc.vector.tensor_scalar(res[:], e[:], stats[:, 1:2], None, ALU.mult)
-            nc.sync.dma_start(out[b * P : (b + 1) * P, :], res[:])
+            rows = out[b * P : (b + 1) * P, :]
+            if b < HALVES - 1:
+                res = sb(f"res{b}", [P, R], F32)
+                nc.vector.tensor_scalar(res[:], e[:], stats[:, 1:2], None, ALU.mult)
+                nc.sync.dma_start(rows, res[:])
+            else:
+                left = sb("res_left", [P, R // 2], F32)
+                right = sb("res_right", [P, R // 2], F32)
+                nc.vector.tensor_scalar(left[:], e[:, 0 : R // 2], stats[:, 1:2], None, ALU.mult)
+                nc.sync.dma_start(rows[:, 0 : R // 2], left[:])
+                nc.scalar.activation(right[:], e[:, R // 2 : R], ACT.Copy, scale=stats[:, 1:2])
+                nc.scalar.dma_start(rows[:, R // 2 : R], right[:])
 
         cast_w(1, nc.scalar.copy, "gate_cols")
         cast_w(2, nc.scalar.copy, "w_raw1_1")

@@ -72,7 +72,7 @@ def tile_picked_zcbow_soft_p_kernel(
         x_table = [load_words("x_table0", x_words[0])]
         offs_t = load_list("offs_t", offs)
         cand_t = load_list("cand_t", cand)
-        x_scale_table = load_scales("x_scale_table", x_scales, nc.vector, (nc.gpsimd, nc.gpsimd, nc.scalar, nc.scalar))
+        x_scale_table = load_scales("x_scale_table", x_scales, nc.vector, (nc.scalar, nc.scalar, nc.gpsimd, nc.gpsimd))
         v_scale_table = sb("v_scale_table", [P, G], U8)
         nc.vector.memset(v_scale_table[:].bitcast(I32), 0)
         nc.scalar.dma_start(v_scale_table[0:P:8, :].bitcast(I32), v_scales[0].bitcast(I32))

@@ -19,9 +19,14 @@ AXIS = mybir.AxisListType
 
 P = 128
 PACK = 4
+QUADRANT = 32
+ROWS = 4
+GROUP = 16
 PASSES = K // (P * PACK)
 TILES = H // P
 HALVES = V // P
+V_SCALE_AT = 8
+GATE_AT = 24
 
 
 def tile_picked_zcbow_soft_p_kernel(
@@ -35,6 +40,11 @@ def tile_picked_zcbow_soft_p_kernel(
         def sb(name, shape, dtype, tag=None):
             return keep.tile(shape, dtype, name=name, tag=tag or name, align_bytes=64)
 
+        def zeroed(name, shape, dtype):
+            tile = sb(name, shape, dtype)
+            nc.vector.memset(tile[:].bitcast(I32), 0)
+            return tile
+
         def load_list(name, src):
             tile = keep.tile(list(src.shape), U16, name=name)
             nc.sync.dma_start(tile[:], src)
@@ -42,28 +52,17 @@ def tile_picked_zcbow_soft_p_kernel(
 
         def load_words(name, src):
             tile = sb(name, [P, T], U32)
-            nc.sync.dma_start(tile[:].bitcast(I32), src.rearrange("p n t -> p (n t)").bitcast(I32))
+            nc.sync.dma_start(tile[:].bitcast(I32), src.rearrange("p n j -> p (n j)").bitcast(I32))
             return tile
 
-        def load_w(name, o, c0, c1):
-            tile = sb(name, [P, PACK, c1 - c0], F32)
-            rows = w1[o * P * PACK : (o + 1) * P * PACK, c0:c1]
+        def load_w(a, o):
+            tile = sb(f"w_raw{a}_{o}", [P, PACK, P], F32)
+            rows = w1[o * P * PACK : (o + 1) * P * PACK, a * P : (a + 1) * P]
             nc.sync.dma_start(tile[:], rows.rearrange("(p j) c -> p j c", j=PACK))
             return tile
 
-        def load_scales(name, src, clear, queues):
-            passes = src.shape[0]
-            tile = sb(name, [P, T], U8)
-            clear.memset(tile[:].bitcast(I32), 0)
-            for q, queue in enumerate(queues):
-                queue.dma_start(
-                    tile[32 * q : 32 * q + 4 * passes, :].bitcast(I32),
-                    src[:, 4 * q : 4 * q + 4, :].bitcast(I32),
-                )
-            return tile
-
         def gather(name, table, offsets, dtype, tag=None):
-            tile = sb(name, [P, offsets.shape[1] * 16], dtype, tag)
+            tile = sb(name, [P, offsets.shape[1] * GROUP], dtype, tag)
             nc.vector.tensor_copy(tile[:], table[:].indirect(offsets))
             return tile
 
@@ -72,55 +71,63 @@ def tile_picked_zcbow_soft_p_kernel(
         x_table = [load_words("x_table0", x_words[0])]
         offs_t = load_list("offs_t", offs)
         cand_t = load_list("cand_t", cand)
-        x_scale_table = load_scales("x_scale_table", x_scales, nc.vector, (nc.scalar, nc.scalar, nc.gpsimd, nc.gpsimd))
-        v_scale_table = sb("v_scale_table", [P, G], U8)
-        nc.vector.memset(v_scale_table[:].bitcast(I32), 0)
-        nc.scalar.dma_start(v_scale_table[0:P:8, :].bitcast(I32), v_scales[0].bitcast(I32))
+
+        x_scale_table = zeroed("x_scale_table", [P, T], U8)
+        for q, queue in enumerate((nc.scalar, nc.scalar, nc.gpsimd, nc.gpsimd)):
+            queue.dma_start(
+                x_scale_table[QUADRANT * q : QUADRANT * q + ROWS * PASSES, :].bitcast(I32),
+                x_scales[:, ROWS * q : ROWS * (q + 1), :].bitcast(I32),
+            )
+        v_scale_table = zeroed("v_scale_table", [P, G], U8)
+        v_scale_rows = v_scales.shape[1]
+        nc.scalar.dma_start(
+            v_scale_table[V_SCALE_AT : V_SCALE_AT + v_scale_rows, :].bitcast(I32), v_scales[0].bitcast(I32)
+        )
         gate_rows = sb("gate_rows", [P, P], F32)
         nc.vector.memset(gate_rows[:], 0.0)
-        warm = sb("warm", [P, 2], F32)
-        nc.vector.memset(warm[:], 0.0)
-        nc.scalar.activation(warm[:, 1:2], warm[:, 0:1], ACT.Exp)
-        v_scale = sb("v_scale", [P, R], U8)
-        nc.vector.memset(v_scale[:].bitcast(I32), 0)
-        w_raw = {}
-        for o in range(PASSES):
-            w_raw[0, o] = load_w(f"w_raw0_{o}", o, 0, P)[:]
-        nc.sync.dma_start(gate_rows[0 : D * HALVES, :], gate[:, 0, :].rearrange("d (b t) -> d b t", t=P))
+        v_scale = zeroed("v_scale", [P, R], U8)
+
+        w_raw = {(0, o): load_w(0, o) for o in range(PASSES)}
+        gate_count = D * HALVES
+        nc.sync.dma_start(
+            gate_rows[GATE_AT : GATE_AT + gate_count, :], gate[:, 0, :].rearrange("d (b t) -> d b t", t=P)
+        )
         x_table.append(load_words("x_table1", x_words[1]))
         for o in range(PASSES):
-            w_raw[1, o] = load_w(f"w_raw1_{o}", o, P, 2 * P)[:]
+            w_raw[1, o] = load_w(1, o)
         pos_t = [load_list(f"pos_t{d}", src) for d, src in enumerate((pos1, pos2, pos3, pos4))]
         for a in range(2, TILES):
             for o in range(PASSES):
-                w_raw[a, o] = load_w(f"w_raw{a}_{o}", o, a * P, (a + 1) * P)[:]
+                w_raw[a, o] = load_w(a, o)
         v_table = load_words("v_table", v_words[0])
 
         gate_turned = psum.tile([P, P], F32, name="gate_turned", tag="h_bank0")
         nc.tensor.transpose(gate_turned[:], gate_rows[:], ident[:])
-        gate_cols = sb("gate_cols", [P, D * HALVES], F32)
-        nc.scalar.copy(gate_cols[:], gate_turned[:, 0 : D * HALVES])
+        gate_cols = sb("gate_cols", [P, gate_count], F32)
+        nc.scalar.copy(gate_cols[:], gate_turned[:, GATE_AT : GATE_AT + gate_count])
         gate_t = []
         for pair in range(D // 2):
             spread = psum.tile([P, 2, V], F32, name=f"gate_spread{pair}", tag=f"h_bank{1 - pair}")
-            for e in range(2):
+            for member in range(2):
                 for b in range(HALVES):
-                    col = (2 * pair + e) * HALVES + b
+                    col = (2 * pair + member) * HALVES + b
                     nc.tensor.transpose(
-                        spread[:, e, b * P : (b + 1) * P], gate_cols[:, col : col + 1].to_broadcast([P, P]), ident[:]
+                        spread[:, member, b * P : (b + 1) * P],
+                        gate_cols[:, col : col + 1].to_broadcast([P, P]),
+                        ident[:],
                     )
             both = sb(f"gate_pair{pair}", [P, 2, V], F32)
             nc.scalar.copy(both[:], spread[:])
             gate_t.extend([both[:, 0, :], both[:, 1, :]])
 
-        w_bf, w_codes, w_scale, h = {}, {}, {}, {}
+        w_bf, w_codes, w_scale, h_acc, h = {}, {}, {}, {}, {}
 
-        def cast_w(a, copy, tag=None):
+        def cast_w(a, tag=None):
             w_bf[a] = sb(f"w_bf{a}", [P, PASSES, P, PACK], BF16, tag)
             for o in range(PASSES):
-                copy(
-                    w_bf[a][:, o, :, :].rearrange("p (c i) j -> p c j i", i=4),
-                    w_raw[a, o].rearrange("p j (c i) -> p c j i", i=4),
+                nc.scalar.copy(
+                    w_bf[a][:, o, :, :].rearrange("p (c n) j -> p c j n", n=4),
+                    w_raw[a, o][:].rearrange("p j (c n) -> p c j n", n=4),
                 )
 
         def quantize_w(a, tag=None):
@@ -132,47 +139,56 @@ def tile_picked_zcbow_soft_p_kernel(
                 in_=w_bf[a][:].rearrange("p o c j -> p (o c j)"),
             )
 
-        acc = {}
-
         def project(a, o, c0, c1):
             if o == 0:
-                acc[a, c0] = psum.tile([P, c1 - c0], F32, name=f"h_acc{a}_{c0}", tag=f"h_bank{(len(acc) + 1) % 2}")
+                bank = f"h_bank{(len(h_acc) + 1) % 2}"
+                h_acc[a, c0] = psum.tile([P, c1 - c0], F32, name=f"h_acc{a}_{c0}", tag=bank)
             nc.tensor.matmul_mx(
-                out=acc[a, c0][:],
+                out=h_acc[a, c0][:],
                 lhsT=w_codes[a][:, o, :].bitcast(FP8X4),
                 lhsT_scale=w_scale[a][:, o, :],
                 rhs=x_codes[o][:, c0:c1].bitcast(FP8X4),
-                rhs_scale=x_scale[4 * o : P, c0:c1],
+                rhs_scale=x_scale[ROWS * o : P, c0:c1],
                 start=(o == 0),
                 stop=(o == PASSES - 1),
             )
 
-        v_scale_spread = gather("v_scale_spread", v_scale_table, cand_t[:], U8)
-        for r in range(4):
-            nc.sync.dma_start(v_scale[r:P:32, :].bitcast(I32), v_scale_spread[8 * r : P : 32, :].bitcast(I32))
+        v_scale_picked = gather("v_scale_picked", v_scale_table, cand_t[:], U8)
+        for q in range(P // QUADRANT):
+            first = V_SCALE_AT + ROWS * q
+            nc.sync.dma_start(
+                v_scale[QUADRANT * q : QUADRANT * q + ROWS, :].bitcast(I32),
+                v_scale_picked[first : first + ROWS, :].bitcast(I32),
+            )
         x_codes = [gather("x_codes0", x_table[0], offs_t[:], U32)]
-        cast_w(0, nc.scalar.copy)
+        cast_w(0)
         x_scale = gather("x_scale", x_scale_table, offs_t[:], U8, "x_table0")
         quantize_w(0)
         x_codes.append(sb("x_codes1", [P, S], U32, "x_scale_table"))
-        for c0 in (0, S // 2):
-            project(0, 0, c0, c0 + S // 2)
-        for c0 in (0, S // 2):
-            c1 = c0 + S // 2
-            nc.vector.tensor_copy(x_codes[1][:, c0:c1], x_table[1][:].indirect(offs_t[:, c0 // 16 : c1 // 16]))
+        list_halves = [(c0, c0 + S // 2) for c0 in (0, S // 2)]
+        for c0, c1 in list_halves:
+            project(0, 0, c0, c1)
+        for c0, c1 in list_halves:
+            nc.vector.tensor_copy(x_codes[1][:, c0:c1], x_table[1][:].indirect(offs_t[:, c0 // GROUP : c1 // GROUP]))
             project(0, 1, c0, c1)
         h[0] = sb("h0", [P, S], F32)
-        for c0 in (0, S // 2):
-            nc.vector.tensor_copy(h[0][:, c0 : c0 + S // 2], acc[0, c0][:])
+        for c0, c1 in list_halves:
+            nc.vector.tensor_copy(h[0][:, c0:c1], h_acc[0, c0][:])
+
+        def finish_h(a, tag=None):
+            for o in range(PASSES):
+                project(a, o, 0, S)
+            h[a] = sb(f"h{a}", [P, S], F32, tag)
+            nc.scalar.copy(h[a][:], h_acc[a, 0][:])
 
         zt = [psum.tile([P, H], F32, name=f"zt{b}") for b in range(HALVES)]
         z_bf = [sb(f"z_bf{b}", [P, 2, P, 2], BF16) for b in range(HALVES)]
 
         def window_term(a, d, tag=None, halves=(0, 1)):
             t0, t1 = halves[0] * P, (halves[-1] + 1) * P
-            term = sb(f"term{a}_{d}_{t0}" if t0 else f"term{a}_{d}", [P, t1 - t0], F32, tag)
+            term = sb(f"term{a}_{d}_{t0}", [P, t1 - t0], F32, tag)
             nc.vector.tensor_tensor(
-                term[:], h[a][:].indirect(pos_t[d][:, t0 // 16 : t1 // 16]), gate_t[d][:, t0:t1], ALU.mult
+                term[:], h[a][:].indirect(pos_t[d][:, t0 // GROUP : t1 // GROUP]), gate_t[d][:, t0:t1], ALU.mult
             )
             for b in halves:
                 nc.tensor.matmul(
@@ -184,15 +200,10 @@ def tile_picked_zcbow_soft_p_kernel(
                     is_transpose=True,
                 )
 
-        def finish_h(a, tag=None):
-            for o in range(PASSES):
-                project(a, o, 0, S)
-            h[a] = sb(f"h{a}", [P, S], F32, tag)
-            nc.scalar.copy(h[a][:], acc[a, 0][:])
-
         def round_z(b, a0, a1):
+            per_tile = P // PACK
             nc.scalar.copy(
-                z_bf[b][:, :, 32 * a0 : 32 * a1, :],
+                z_bf[b][:, :, per_tile * a0 : per_tile * a1, :],
                 zt[b][:, a0 * P : a1 * P].rearrange("t (p u e) -> t u p e", u=2, e=2),
             )
 
@@ -221,33 +232,33 @@ def tile_picked_zcbow_soft_p_kernel(
             return y
 
         def softmax(b, y):
-            stats = sb(f"stats{b}", [P, 4], F32)
+            sums = sb(f"sums{b}", [P, 4], F32)
             neg_max = sb(f"neg_max{b}", [P, 1], F32)
             nc.vector.tensor_reduce(neg_max[:], y[:], AXIS.X, ALU.max, negate=True)
-            e = sb(f"e{b}", [P, R], F32)
-            nc.scalar.activation(e[:], y[:], ACT.Exp, bias=neg_max[:], accum_out=stats[:, 0:1])
-            nc.vector.reciprocal(stats[:, 1:2], stats[:, 0:1])
+            exps = sb(f"exps{b}", [P, R], F32)
+            nc.scalar.activation(exps[:], y[:], ACT.Exp, bias=neg_max[:], accum_out=sums[:, 0:1])
+            nc.vector.reciprocal(sums[:, 1:2], sums[:, 0:1])
             rows = out[b * P : (b + 1) * P, :]
             if b < HALVES - 1:
                 res = sb(f"res{b}", [P, R], F32)
-                nc.vector.tensor_scalar(res[:], e[:], stats[:, 1:2], None, ALU.mult)
+                nc.vector.tensor_scalar(res[:], exps[:], sums[:, 1:2], None, ALU.mult)
                 nc.sync.dma_start(rows, res[:])
             else:
                 left = sb("res_left", [P, R // 2], F32)
                 right = sb("res_right", [P, R // 2], F32)
-                nc.vector.tensor_scalar(left[:], e[:, 0 : R // 2], stats[:, 1:2], None, ALU.mult)
+                nc.vector.tensor_scalar(left[:], exps[:, 0 : R // 2], sums[:, 1:2], None, ALU.mult)
                 nc.sync.dma_start(rows[:, 0 : R // 2], left[:])
-                nc.scalar.activation(right[:], e[:, R // 2 : R], ACT.Copy, scale=stats[:, 1:2])
+                nc.scalar.activation(right[:], exps[:, R // 2 : R], ACT.Copy, scale=sums[:, 1:2])
                 nc.scalar.dma_start(rows[:, R // 2 : R], right[:])
 
-        cast_w(1, nc.scalar.copy, "gate_cols")
-        cast_w(2, nc.scalar.copy, "w_raw1_1")
+        cast_w(1, "gate_cols")
+        cast_w(2, "w_raw1_1")
         quantize_w(1, "w_codes0")
         finish_h(1, "w_raw2_1")
         window_term(0, 0)
         window_term(0, 1, "gate_cols")
-        quantize_w(2, "term0_0")
-        cast_w(3, nc.scalar.copy, "w_codes0")
+        quantize_w(2, "term0_0_0")
+        cast_w(3, "w_codes0")
         finish_h(2, "w_raw3_1")
         window_term(0, 2)
         window_term(0, 3)
@@ -260,13 +271,14 @@ def tile_picked_zcbow_soft_p_kernel(
         window_term(2, 0, "w_codes0")
         for d in range(1, D):
             window_term(2, d)
+        last = TILES - 1
         for b in range(HALVES):
-            round_z(b, 0, 3)
+            round_z(b, 0, last)
         for b in range(HALVES):
             for d in range(D):
-                window_term(3, d, halves=(b,))
-            round_z(b, 3, 4)
-        v_codes = gather("v_codes", v_table, cand_t[:], U32, "term3_2_128")
-        y = [score(b) for b in range(HALVES)]
+                window_term(last, d, halves=(b,))
+            round_z(b, last, TILES)
+        v_codes = gather("v_codes", v_table, cand_t[:], U32, f"term{last}_{D - 2}_{P}")
+        scores = [score(b) for b in range(HALVES)]
         for b in range(HALVES):
-            softmax(b, y[b])
+            softmax(b, scores[b])

@@ -68,30 +68,30 @@ def tile_picked_zcbow_soft_p_kernel(
 
         ident = sb("ident", [P, P], F32)
         make_identity(nc, ident[:])
+        cand_t = load_list("cand_t", cand)
         x_table = [load_words("x_table0", x_words[0])]
         offs_t = load_list("offs_t", offs)
-        cand_t = load_list("cand_t", cand)
 
+        v_scale_table = zeroed("v_scale_table", [P, G], U8)
+        v_scale_rows = v_scales.shape[1]
+        nc.scalar.dma_start(
+            v_scale_table[V_SCALE_AT : V_SCALE_AT + v_scale_rows, :].bitcast(I32), v_scales[0].bitcast(I32)
+        )
         x_scale_table = zeroed("x_scale_table", [P, T], U8)
         for q, queue in enumerate((nc.scalar, nc.scalar, nc.gpsimd, nc.gpsimd)):
             queue.dma_start(
                 x_scale_table[QUADRANT * q : QUADRANT * q + ROWS * PASSES, :].bitcast(I32),
                 x_scales[:, ROWS * q : ROWS * (q + 1), :].bitcast(I32),
             )
-        v_scale_table = zeroed("v_scale_table", [P, G], U8)
-        v_scale_rows = v_scales.shape[1]
-        nc.scalar.dma_start(
-            v_scale_table[V_SCALE_AT : V_SCALE_AT + v_scale_rows, :].bitcast(I32), v_scales[0].bitcast(I32)
-        )
         gate_rows = sb("gate_rows", [P, P], F32)
         nc.vector.memset(gate_rows[:], 0.0)
         v_scale = zeroed("v_scale", [P, R], U8)
 
-        w_raw = {(0, o): load_w(0, o) for o in range(PASSES)}
         gate_count = D * HALVES
         nc.sync.dma_start(
             gate_rows[GATE_AT : GATE_AT + gate_count, :], gate[:, 0, :].rearrange("d (b t) -> d b t", t=P)
         )
+        w_raw = {(0, o): load_w(0, o) for o in range(PASSES)}
         x_table.append(load_words("x_table1", x_words[1]))
         for o in range(PASSES):
             w_raw[1, o] = load_w(1, o)
@@ -101,13 +101,13 @@ def tile_picked_zcbow_soft_p_kernel(
                 w_raw[a, o] = load_w(a, o)
         v_table = load_words("v_table", v_words[0])
 
-        gate_turned = psum.tile([P, P], F32, name="gate_turned", tag="h_bank0")
+        gate_turned = psum.tile([P, P], F32, name="gate_turned", tag="h_bank1")
         nc.tensor.transpose(gate_turned[:], gate_rows[:], ident[:])
         gate_cols = sb("gate_cols", [P, gate_count], F32)
         nc.scalar.copy(gate_cols[:], gate_turned[:, GATE_AT : GATE_AT + gate_count])
         gate_t = []
         for pair in range(D // 2):
-            spread = psum.tile([P, 2, V], F32, name=f"gate_spread{pair}", tag=f"h_bank{1 - pair}")
+            spread = psum.tile([P, 2, V], F32, name=f"gate_spread{pair}", tag=f"turned{pair}")
             for member in range(2):
                 for b in range(HALVES):
                     col = (2 * pair + member) * HALVES + b
@@ -141,7 +141,7 @@ def tile_picked_zcbow_soft_p_kernel(
 
         def project(a, o, c0, c1):
             if o == 0:
-                bank = f"h_bank{(len(h_acc) + 1) % 2}"
+                bank = ["h_bank1", "y0", "h_bank0", "h_bank1", "h_bank0", "h_bank1"][len(h_acc)]
                 h_acc[a, c0] = psum.tile([P, c1 - c0], F32, name=f"h_acc{a}_{c0}", tag=bank)
             nc.tensor.matmul_mx(
                 out=h_acc[a, c0][:],
@@ -166,14 +166,18 @@ def tile_picked_zcbow_soft_p_kernel(
         quantize_w(0)
         x_codes.append(sb("x_codes1", [P, S], U32, "x_scale_table"))
         list_halves = [(c0, c0 + S // 2) for c0 in (0, S // 2)]
-        for c0, c1 in list_halves:
-            project(0, 0, c0, c1)
-        for c0, c1 in list_halves:
-            nc.vector.tensor_copy(x_codes[1][:, c0:c1], x_table[1][:].indirect(offs_t[:, c0 // GROUP : c1 // GROUP]))
-            project(0, 1, c0, c1)
+        pieces = [[(0, 256)], [(256, 384), (384, 512)]]
+        for half in pieces:
+            for c0, c1 in half:
+                project(0, 0, c0, c1)
+        for (g0, g1), half in zip(list_halves, pieces):
+            nc.vector.tensor_copy(x_codes[1][:, g0:g1], x_table[1][:].indirect(offs_t[:, g0 // GROUP : g1 // GROUP]))
+            for c0, c1 in half:
+                project(0, 1, c0, c1)
         h[0] = sb("h0", [P, S], F32)
-        for c0, c1 in list_halves:
-            nc.vector.tensor_copy(h[0][:, c0:c1], h_acc[0, c0][:])
+        nc.vector.tensor_copy(h[0][:, 0:256], h_acc[0, 0][:])
+        nc.vector.tensor_copy(h[0][:, 256:384], h_acc[0, 256][:])
+        nc.vector.tensor_copy(h[0][:, 384:512], h_acc[0, 384][:])
 
         def finish_h(a, tag=None):
             for o in range(PASSES):
@@ -248,7 +252,7 @@ def tile_picked_zcbow_soft_p_kernel(
                 right = sb("res_right", [P, R // 2], F32)
                 nc.vector.tensor_scalar(left[:], exps[:, 0 : R // 2], sums[:, 1:2], None, ALU.mult)
                 nc.sync.dma_start(rows[:, 0 : R // 2], left[:])
-                nc.scalar.activation(right[:], exps[:, R // 2 : R], ACT.Copy, scale=sums[:, 1:2])
+                nc.vector.tensor_scalar(right[:], exps[:, R // 2 : R], sums[:, 1:2], None, ALU.mult)
                 nc.scalar.dma_start(rows[:, R // 2 : R], right[:])
 
         cast_w(1, "gate_cols")
@@ -274,8 +278,10 @@ def tile_picked_zcbow_soft_p_kernel(
         last = TILES - 1
         for b in range(HALVES):
             round_z(b, 0, last)
+        for d in range(D // 2):
+            window_term(last, d)
         for b in range(HALVES):
-            for d in range(D):
+            for d in range(D // 2, D):
                 window_term(last, d, halves=(b,))
             round_z(b, last, TILES)
         v_codes = gather("v_codes", v_table, cand_t[:], U32, f"term{last}_{D - 2}_{P}")

@@ -25,8 +25,9 @@ GROUP = 16
 PASSES = K // (P * PACK)
 TILES = H // P
 HALVES = V // P
-V_SCALE_AT = 8
+V_SCALE_AT, V_SCALE_STEP = 10, 7
 GATE_AT = 24
+WHOLE_TERMS = 1
 
 
 def tile_picked_zcbow_soft_p_kernel(
@@ -40,9 +41,9 @@ def tile_picked_zcbow_soft_p_kernel(
         def sb(name, shape, dtype, tag=None):
             return keep.tile(shape, dtype, name=name, tag=tag or name, align_bytes=64)
 
-        def zeroed(name, shape, dtype):
+        def zeroed(name, shape, dtype, engine):
             tile = sb(name, shape, dtype)
-            nc.vector.memset(tile[:].bitcast(I32), 0)
+            engine.memset(tile[:].bitcast(I32), 0)
             return tile
 
         def load_list(name, src):
@@ -66,26 +67,25 @@ def tile_picked_zcbow_soft_p_kernel(
             nc.vector.tensor_copy(tile[:], table[:].indirect(offsets))
             return tile
 
-        ident = sb("ident", [P, P], F32)
-        make_identity(nc, ident[:])
+        v_scale_table = zeroed("v_scale_table", [P, G], U8, nc.gpsimd)
+        ident = zeroed("ident", [P, P], F32, nc.vector)
+        make_identity(nc, ident[:], nomemset=True)
         cand_t = load_list("cand_t", cand)
         x_table = [load_words("x_table0", x_words[0])]
         offs_t = load_list("offs_t", offs)
-
-        v_scale_table = zeroed("v_scale_table", [P, G], U8)
         v_scale_rows = v_scales.shape[1]
         nc.scalar.dma_start(
-            v_scale_table[V_SCALE_AT : V_SCALE_AT + v_scale_rows, :].bitcast(I32), v_scales[0].bitcast(I32)
+            v_scale_table[V_SCALE_AT : V_SCALE_AT + V_SCALE_STEP * v_scale_rows : V_SCALE_STEP, :].bitcast(I32),
+            v_scales[0].bitcast(I32),
         )
-        x_scale_table = zeroed("x_scale_table", [P, T], U8)
+        x_scale_table = zeroed("x_scale_table", [P, T], U8, nc.vector)
         for q, queue in enumerate((nc.scalar, nc.scalar, nc.gpsimd, nc.gpsimd)):
             queue.dma_start(
                 x_scale_table[QUADRANT * q : QUADRANT * q + ROWS * PASSES, :].bitcast(I32),
                 x_scales[:, ROWS * q : ROWS * (q + 1), :].bitcast(I32),
             )
-        gate_rows = sb("gate_rows", [P, P], F32)
-        nc.vector.memset(gate_rows[:], 0.0)
-        v_scale = zeroed("v_scale", [P, R], U8)
+        gate_rows = zeroed("gate_rows", [P, P], F32, nc.vector)
+        v_scale = zeroed("v_scale", [P, R], U8, nc.vector)
 
         gate_count = D * HALVES
         nc.sync.dma_start(
@@ -105,7 +105,7 @@ def tile_picked_zcbow_soft_p_kernel(
         nc.tensor.transpose(gate_turned[:], gate_rows[:], ident[:])
         gate_cols = sb("gate_cols", [P, gate_count], F32)
         nc.scalar.copy(gate_cols[:], gate_turned[:, GATE_AT : GATE_AT + gate_count])
-        gate_t = []
+        spreads = []
         for pair in range(D // 2):
             spread = psum.tile([P, 2, V], F32, name=f"gate_spread{pair}", tag=f"turned{pair}")
             for member in range(2):
@@ -116,9 +116,7 @@ def tile_picked_zcbow_soft_p_kernel(
                         gate_cols[:, col : col + 1].to_broadcast([P, P]),
                         ident[:],
                     )
-            both = sb(f"gate_pair{pair}", [P, 2, V], F32)
-            nc.scalar.copy(both[:], spread[:])
-            gate_t.extend([both[:, 0, :], both[:, 1, :]])
+            spreads.append(spread)
 
         w_bf, w_codes, w_scale, h_acc, h = {}, {}, {}, {}, {}
 
@@ -139,9 +137,8 @@ def tile_picked_zcbow_soft_p_kernel(
                 in_=w_bf[a][:].rearrange("p o c j -> p (o c j)"),
             )
 
-        def project(a, o, c0, c1):
+        def project(a, o, c0, c1, bank):
             if o == 0:
-                bank = ["h_bank1", "y0", "h_bank0", "h_bank1", "h_bank0", "h_bank1"][len(h_acc)]
                 h_acc[a, c0] = psum.tile([P, c1 - c0], F32, name=f"h_acc{a}_{c0}", tag=bank)
             nc.tensor.matmul_mx(
                 out=h_acc[a, c0][:],
@@ -155,33 +152,37 @@ def tile_picked_zcbow_soft_p_kernel(
 
         v_scale_picked = gather("v_scale_picked", v_scale_table, cand_t[:], U8)
         for q in range(P // QUADRANT):
-            first = V_SCALE_AT + ROWS * q
+            first = V_SCALE_AT + V_SCALE_STEP * ROWS * q
             nc.sync.dma_start(
                 v_scale[QUADRANT * q : QUADRANT * q + ROWS, :].bitcast(I32),
-                v_scale_picked[first : first + ROWS, :].bitcast(I32),
+                v_scale_picked[first : first + V_SCALE_STEP * ROWS : V_SCALE_STEP, :].bitcast(I32),
             )
         x_codes = [gather("x_codes0", x_table[0], offs_t[:], U32)]
         cast_w(0)
+        gate_all = sb("gate_all", [P, D, V], F32, "w_raw0_1")
+        for pair, spread in enumerate(spreads):
+            nc.scalar.copy(gate_all[:, 2 * pair : 2 * pair + 2, :], spread[:])
         x_scale = gather("x_scale", x_scale_table, offs_t[:], U8, "x_table0")
         quantize_w(0)
         x_codes.append(sb("x_codes1", [P, S], U32, "x_scale_table"))
-        list_halves = [(c0, c0 + S // 2) for c0 in (0, S // 2)]
-        pieces = [[(0, 256)], [(256, 384), (384, 512)]]
-        for half in pieces:
-            for c0, c1 in half:
-                project(0, 0, c0, c1)
-        for (g0, g1), half in zip(list_halves, pieces):
-            nc.vector.tensor_copy(x_codes[1][:, g0:g1], x_table[1][:].indirect(offs_t[:, g0 // GROUP : g1 // GROUP]))
-            for c0, c1 in half:
-                project(0, 1, c0, c1)
+        half, quarter = S // 2, S // 4
+        groups = [(0, half, "h_bank1"), (half, half + quarter, "y0"), (half + quarter, S, "h_bank0")]
+        for c0, c1, bank in groups:
+            project(0, 0, c0, c1, bank)
+        for g0 in (0, half):
+            nc.vector.tensor_copy(
+                x_codes[1][:, g0 : g0 + half], x_table[1][:].indirect(offs_t[:, g0 // GROUP : (g0 + half) // GROUP])
+            )
+            for c0, c1, bank in groups:
+                if g0 <= c0 < g0 + half:
+                    project(0, 1, c0, c1, bank)
         h[0] = sb("h0", [P, S], F32)
-        nc.vector.tensor_copy(h[0][:, 0:256], h_acc[0, 0][:])
-        nc.vector.tensor_copy(h[0][:, 256:384], h_acc[0, 256][:])
-        nc.vector.tensor_copy(h[0][:, 384:512], h_acc[0, 384][:])
+        for c0, c1, bank in groups:
+            nc.vector.tensor_copy(h[0][:, c0:c1], h_acc[0, c0][:])
 
         def finish_h(a, tag=None):
             for o in range(PASSES):
-                project(a, o, 0, S)
+                project(a, o, 0, S, f"h_bank{a % 2}")
             h[a] = sb(f"h{a}", [P, S], F32, tag)
             nc.scalar.copy(h[a][:], h_acc[a, 0][:])
 
@@ -192,7 +193,7 @@ def tile_picked_zcbow_soft_p_kernel(
             t0, t1 = halves[0] * P, (halves[-1] + 1) * P
             term = sb(f"term{a}_{d}_{t0}", [P, t1 - t0], F32, tag)
             nc.vector.tensor_tensor(
-                term[:], h[a][:].indirect(pos_t[d][:, t0 // GROUP : t1 // GROUP]), gate_t[d][:, t0:t1], ALU.mult
+                term[:], h[a][:].indirect(pos_t[d][:, t0 // GROUP : t1 // GROUP]), gate_all[:, d, t0:t1], ALU.mult
             )
             for b in halves:
                 nc.tensor.matmul(
@@ -278,13 +279,13 @@ def tile_picked_zcbow_soft_p_kernel(
         last = TILES - 1
         for b in range(HALVES):
             round_z(b, 0, last)
-        for d in range(D // 2):
+        for d in range(WHOLE_TERMS):
             window_term(last, d)
         for b in range(HALVES):
-            for d in range(D // 2, D):
+            for d in range(WHOLE_TERMS, D):
                 window_term(last, d, halves=(b,))
             round_z(b, last, TILES)
-        v_codes = gather("v_codes", v_table, cand_t[:], U32, f"term{last}_{D - 2}_{P}")
+        v_codes = gather("v_codes", v_table, cand_t[:], U32, f"term{last}_0_0")
         scores = [score(b) for b in range(HALVES)]
         for b in range(HALVES):
             softmax(b, scores[b])

@@ -27,7 +27,7 @@ TILES = H // P
 HALVES = V // P
 V_SCALE_AT, V_SCALE_STEP = 10, 7
 GATE_AT = 24
-WHOLE_TERMS = 1
+WHOLE_TERMS = 0
 
 
 def tile_picked_zcbow_soft_p_kernel(
@@ -195,15 +195,31 @@ def tile_picked_zcbow_soft_p_kernel(
             nc.vector.tensor_tensor(
                 term[:], h[a][:].indirect(pos_t[d][:, t0 // GROUP : t1 // GROUP]), gate_all[:, d, t0:t1], ALU.mult
             )
-            for b in halves:
+            add_term(a, d, term[:], halves)
+
+        def add_term(a, d, term, halves):
+            for n, b in enumerate(halves):
                 nc.tensor.matmul(
                     zt[b][:, a * P : (a + 1) * P],
-                    term[:, b * P - t0 : (b + 1) * P - t0],
+                    term[:, n * P : (n + 1) * P],
                     ident[:],
                     start=(d == 0),
                     stop=(d == D - 1),
                     is_transpose=True,
                 )
+
+        def fetch(a, d0):
+            picked = sb(f"picked{a}", [P, D - d0, V], F32)
+            for d in range(d0, D):
+                nc.scalar.activation(picked[:, d - d0, :], h[a][:].indirect(pos_t[d][:]), ACT.Copy)
+            return picked
+
+        def weigh(a, d0, picked, halves=(0, 1)):
+            t0, t1 = halves[0] * P, (halves[-1] + 1) * P
+            terms = sb(f"weighed{a}_{t0}", [P, D - d0, t1 - t0], F32)
+            nc.vector.tensor_tensor(terms[:], picked[:, :, t0:t1], gate_all[:, d0:D, t0:t1], ALU.mult)
+            for d in range(d0, D):
+                add_term(a, d, terms[:, d - d0, :], halves)
 
         def round_z(b, a0, a1):
             per_tile = P // PACK
@@ -212,7 +228,7 @@ def tile_picked_zcbow_soft_p_kernel(
                 zt[b][:, a0 * P : a1 * P].rearrange("t (p u e) -> t u p e", u=2, e=2),
             )
 
-        def score(b):
+        def pack_z(b):
             words = z_bf[b][:].rearrange("t u p e -> t (u p e)").bitcast(F32)
             turned = psum.tile([P, 2, P], F32, name=f"turned{b}")
             for u in range(2):
@@ -224,17 +240,18 @@ def tile_picked_zcbow_soft_p_kernel(
             z_codes = sb(f"z_codes{b}", [P, P], U32)
             z_scale = sb(f"z_scale{b}", [P, P], U8)
             nc.vector.quantize_mx(out=z_codes[:].bitcast(FP8X4), scales=z_scale[:], in_=z_in[:])
-            y = psum.tile([P, R], F32, name=f"y{b}")
+            return z_codes, z_scale
+
+        def score(y, z_codes, z_scale, c0, c1):
             nc.tensor.matmul_mx(
-                out=y[:],
+                out=y[:, c0:c1],
                 lhsT=z_codes[:].bitcast(FP8X4),
                 lhsT_scale=z_scale[:],
-                rhs=v_codes[:].bitcast(FP8X4),
-                rhs_scale=v_scale[:],
+                rhs=v_codes[:, c0:c1].bitcast(FP8X4),
+                rhs_scale=v_scale[:, c0:c1],
                 start=True,
                 stop=True,
             )
-            return y
 
         def softmax(b, y):
             sums = sb(f"sums{b}", [P, 4], F32)
@@ -257,35 +274,46 @@ def tile_picked_zcbow_soft_p_kernel(
                 nc.scalar.dma_start(rows[:, R // 2 : R], right[:])
 
         cast_w(1, "gate_cols")
+        picked0 = fetch(0, 3)
         cast_w(2, "w_raw1_1")
         quantize_w(1, "w_codes0")
         finish_h(1, "w_raw2_1")
+        picked1 = fetch(1, 3)
         window_term(0, 0)
         window_term(0, 1, "gate_cols")
         quantize_w(2, "term0_0_0")
         cast_w(3, "w_codes0")
         finish_h(2, "w_raw3_1")
         window_term(0, 2)
-        window_term(0, 3)
+        weigh(0, 3, picked0)
         window_term(1, 0, "w_raw1_1")
         window_term(1, 1)
         quantize_w(3, "w_raw1_1")
+        picked2 = fetch(2, 2)
         finish_h(3)
+        picked3 = fetch(3, 3)
         window_term(1, 2)
-        window_term(1, 3)
+        weigh(1, 3, picked1)
         window_term(2, 0, "w_codes0")
-        for d in range(1, D):
-            window_term(2, d)
+        window_term(2, 1)
+        weigh(2, 2, picked2)
         last = TILES - 1
         for b in range(HALVES):
             round_z(b, 0, last)
         for d in range(WHOLE_TERMS):
             window_term(last, d)
         for b in range(HALVES):
-            for d in range(WHOLE_TERMS, D):
+            for d in range(WHOLE_TERMS, D - 1):
                 window_term(last, d, halves=(b,))
+            weigh(last, D - 1, picked3, halves=(b,))
             round_z(b, last, TILES)
-        v_codes = gather("v_codes", v_table, cand_t[:], U32, f"term{last}_0_0")
-        scores = [score(b) for b in range(HALVES)]
+        scores = [psum.tile([P, R], F32, name=f"y{b}") for b in range(HALVES)]
+        packed0 = pack_z(0)
+        v_codes = sb("v_codes", [P, R], U32, f"term{last}_0_0")
+        for c0 in (0, R // 2):
+            c1 = c0 + R // 2
+            nc.vector.tensor_copy(v_codes[:, c0:c1], v_table[:].indirect(cand_t[:, c0 // GROUP : c1 // GROUP]))
+            score(scores[0], *packed0, c0, c1)
+        score(scores[1], *pack_z(1), 0, R)
         for b in range(HALVES):
             softmax(b, scores[b])

@@ -120,9 +120,10 @@ def tile_picked_zcbow_soft_p_kernel(
 
         w_bf, w_codes, w_scale, h_acc, h = {}, {}, {}, {}, {}
 
-        def cast_w(a, tag=None):
-            w_bf[a] = sb(f"w_bf{a}", [P, PASSES, P, PACK], BF16, tag)
-            for o in range(PASSES):
+        def cast_w(a, tag=None, passes=(0, 1)):
+            if passes[0] == 0:
+                w_bf[a] = sb(f"w_bf{a}", [P, PASSES, P, PACK], BF16, tag)
+            for o in passes:
                 nc.scalar.copy(
                     w_bf[a][:, o, :, :].rearrange("p (c n) j -> p c j n", n=4),
                     w_raw[a, o][:].rearrange("p j (c n) -> p c j n", n=4),
@@ -187,7 +188,7 @@ def tile_picked_zcbow_soft_p_kernel(
             nc.scalar.copy(h[a][:], h_acc[a, 0][:])
 
         zt = [psum.tile([P, H], F32, name=f"zt{b}") for b in range(HALVES)]
-        z_bf = [sb(f"z_bf{b}", [P, 2, P, 2], BF16) for b in range(HALVES)]
+        z_bf = {}
 
         def window_term(a, d, tag=None, halves=(0, 1)):
             t0, t1 = halves[0] * P, (halves[-1] + 1) * P
@@ -221,8 +222,10 @@ def tile_picked_zcbow_soft_p_kernel(
             for d in range(d0, D):
                 add_term(a, d, terms[:, d - d0, :], halves)
 
-        def round_z(b, a0, a1):
+        def round_z(b, a0, a1, tag=None):
             per_tile = P // PACK
+            if a0 == 0:
+                z_bf[b] = sb(f"z_bf{b}", [P, 2, P, 2], BF16, tag)
             nc.scalar.copy(
                 z_bf[b][:, :, per_tile * a0 : per_tile * a1, :],
                 zt[b][:, a0 * P : a1 * P].rearrange("t (p u e) -> t u p e", u=2, e=2),
@@ -274,32 +277,33 @@ def tile_picked_zcbow_soft_p_kernel(
                 nc.scalar.dma_start(rows[:, R // 2 : R], right[:])
 
         cast_w(1, "gate_cols")
+        cast_w(2, "w_raw1_0", passes=(0,))
         picked0 = fetch(0, 3)
-        cast_w(2, "w_raw1_1")
+        cast_w(2, passes=(1,))
         quantize_w(1, "w_codes0")
         finish_h(1, "w_raw2_1")
         picked1 = fetch(1, 3)
         window_term(0, 0)
-        window_term(0, 1, "gate_cols")
-        quantize_w(2, "term0_0_0")
+        window_term(0, 1, "w_raw1_1")
+        quantize_w(2)
         cast_w(3, "w_codes0")
         finish_h(2, "w_raw3_1")
         window_term(0, 2)
         weigh(0, 3, picked0)
-        window_term(1, 0, "w_raw1_1")
+        window_term(1, 0)
         window_term(1, 1)
-        quantize_w(3, "w_raw1_1")
+        quantize_w(3)
         picked2 = fetch(2, 2)
         finish_h(3)
         picked3 = fetch(3, 3)
         window_term(1, 2)
         weigh(1, 3, picked1)
-        window_term(2, 0, "w_codes0")
+        window_term(2, 0)
         window_term(2, 1)
         weigh(2, 2, picked2)
         last = TILES - 1
-        for b in range(HALVES):
-            round_z(b, 0, last)
+        round_z(0, 0, last, "w_codes3")
+        round_z(1, 0, last, "w_scale3")
         for d in range(WHOLE_TERMS):
             window_term(last, d)
         for b in range(HALVES):

@@ -120,10 +120,9 @@ def tile_picked_zcbow_soft_p_kernel(
 
         w_bf, w_codes, w_scale, h_acc, h = {}, {}, {}, {}, {}
 
-        def cast_w(a, tag=None, passes=(0, 1)):
-            if passes[0] == 0:
-                w_bf[a] = sb(f"w_bf{a}", [P, PASSES, P, PACK], BF16, tag)
-            for o in passes:
+        def cast_w(a, tag=None):
+            w_bf[a] = sb(f"w_bf{a}", [P, PASSES, P, PACK], BF16, tag)
+            for o in range(PASSES):
                 nc.scalar.copy(
                     w_bf[a][:, o, :, :].rearrange("p (c n) j -> p c j n", n=4),
                     w_raw[a, o][:].rearrange("p j (c n) -> p c j n", n=4),
@@ -277,9 +276,8 @@ def tile_picked_zcbow_soft_p_kernel(
                 nc.scalar.dma_start(rows[:, R // 2 : R], right[:])
 
         cast_w(1, "gate_cols")
-        cast_w(2, "w_raw1_0", passes=(0,))
         picked0 = fetch(0, 3)
-        cast_w(2, passes=(1,))
+        cast_w(2, "w_raw1_0")
         quantize_w(1, "w_codes0")
         finish_h(1, "w_raw2_1")
         picked1 = fetch(1, 3)

@@ -118,11 +118,12 @@ def tile_picked_zcbow_soft_p_kernel(
                     )
             spreads.append(spread)
 
-        w_bf, w_codes, w_scale, h_acc, h = {}, {}, {}, {}, {}
+        w_bf, w_codes, w_scale, h_acc, h, by_pass = {}, {}, {}, {}, {}, {}
 
-        def cast_w(a, tag=None):
-            w_bf[a] = sb(f"w_bf{a}", [P, PASSES, P, PACK], BF16, tag)
-            for o in range(PASSES):
+        def cast_w(a, tag=None, passes=(0, 1)):
+            if passes[0] == 0:
+                w_bf[a] = sb(f"w_bf{a}", [P, PASSES, P, PACK], BF16, tag)
+            for o in passes:
                 nc.scalar.copy(
                     w_bf[a][:, o, :, :].rearrange("p (c n) j -> p c j n", n=4),
                     w_raw[a, o][:].rearrange("p j (c n) -> p c j n", n=4),
@@ -137,13 +138,21 @@ def tile_picked_zcbow_soft_p_kernel(
                 in_=w_bf[a][:].rearrange("p o c j -> p (o c j)"),
             )
 
+        def quantize_pass(a, o, tag=None):
+            codes = sb(f"w_codes{a}_{o}", [P, P], U32, tag)
+            scale = sb(f"w_scale{a}_{o}", [P, P], U8)
+            nc.vector.quantize_mx(
+                out=codes[:].bitcast(FP8X4), scales=scale[:], in_=w_bf[a][:, o, :, :].rearrange("p c j -> p (c j)")
+            )
+            by_pass[a, o] = codes, scale
+
         def project(a, o, c0, c1, bank):
             if o == 0:
                 h_acc[a, c0] = psum.tile([P, c1 - c0], F32, name=f"h_acc{a}_{c0}", tag=bank)
             nc.tensor.matmul_mx(
                 out=h_acc[a, c0][:],
-                lhsT=w_codes[a][:, o, :].bitcast(FP8X4),
-                lhsT_scale=w_scale[a][:, o, :],
+                lhsT=(by_pass[a, o][0][:] if a == 1 else w_codes[a][:, o, :]).bitcast(FP8X4),
+                lhsT_scale=by_pass[a, o][1][:] if a == 1 else w_scale[a][:, o, :],
                 rhs=x_codes[o][:, c0:c1].bitcast(FP8X4),
                 rhs_scale=x_scale[ROWS * o : P, c0:c1],
                 start=(o == 0),
@@ -278,14 +287,16 @@ def tile_picked_zcbow_soft_p_kernel(
         cast_w(1, "gate_cols")
         picked0 = fetch(0, 3)
         cast_w(2, "w_raw1_0")
-        quantize_w(1, "w_codes0")
+        quantize_pass(1, 0, "w_codes0")
+        quantize_pass(1, 1, "w_scale0")
         finish_h(1, "w_raw2_1")
         picked1 = fetch(1, 3)
         window_term(0, 0)
         window_term(0, 1, "w_raw1_1")
         quantize_w(2)
-        cast_w(3, "w_codes0")
-        finish_h(2, "w_raw3_1")
+        cast_w(3, "w_scale0", passes=(0,))
+        finish_h(2, "w_raw3_0")
+        cast_w(3, passes=(1,))
         window_term(0, 2)
         weigh(0, 3, picked0)
         window_term(1, 0)
@@ -296,7 +307,7 @@ def tile_picked_zcbow_soft_p_kernel(
         picked3 = fetch(3, 3)
         window_term(1, 2)
         weigh(1, 3, picked1)
-        window_term(2, 0)
+        window_term(2, 0, "w_raw3_1")
         window_term(2, 1)
         weigh(2, 2, picked2)
         last = TILES - 1

@@ -151,8 +151,8 @@ def tile_picked_zcbow_soft_p_kernel(
                 h_acc[a, c0] = psum.tile([P, c1 - c0], F32, name=f"h_acc{a}_{c0}", tag=bank)
             nc.tensor.matmul_mx(
                 out=h_acc[a, c0][:],
-                lhsT=(by_pass[a, o][0][:] if a == 1 else w_codes[a][:, o, :]).bitcast(FP8X4),
-                lhsT_scale=by_pass[a, o][1][:] if a == 1 else w_scale[a][:, o, :],
+                lhsT=(by_pass[a, o][0][:] if a % 2 else w_codes[a][:, o, :]).bitcast(FP8X4),
+                lhsT_scale=by_pass[a, o][1][:] if a % 2 else w_scale[a][:, o, :],
                 rhs=x_codes[o][:, c0:c1].bitcast(FP8X4),
                 rhs_scale=x_scale[ROWS * o : P, c0:c1],
                 start=(o == 0),
@@ -277,12 +277,13 @@ def tile_picked_zcbow_soft_p_kernel(
                 nc.vector.tensor_scalar(res[:], exps[:], sums[:, 1:2], None, ALU.mult)
                 nc.sync.dma_start(rows, res[:])
             else:
-                left = sb("res_left", [P, R // 2], F32)
-                right = sb("res_right", [P, R // 2], F32)
-                nc.vector.tensor_scalar(left[:], exps[:, 0 : R // 2], sums[:, 1:2], None, ALU.mult)
-                nc.sync.dma_start(rows[:, 0 : R // 2], left[:])
-                nc.vector.tensor_scalar(right[:], exps[:, R // 2 : R], sums[:, 1:2], None, ALU.mult)
-                nc.scalar.dma_start(rows[:, R // 2 : R], right[:])
+                cut = 320
+                left = sb("res_left", [P, cut], F32)
+                right = sb("res_right", [P, R - cut], F32)
+                nc.vector.tensor_scalar(left[:], exps[:, 0:cut], sums[:, 1:2], None, ALU.mult)
+                nc.sync.dma_start(rows[:, 0:cut], left[:])
+                nc.scalar.activation(right[:], exps[:, cut:R], ACT.Copy, scale=sums[:, 1:2])
+                nc.scalar.dma_start(rows[:, cut:R], right[:])
 
         cast_w(1, "gate_cols")
         picked0 = fetch(0, 3)
@@ -300,8 +301,9 @@ def tile_picked_zcbow_soft_p_kernel(
         window_term(0, 2)
         weigh(0, 3, picked0)
         window_term(1, 0)
+        quantize_pass(3, 0)
         window_term(1, 1)
-        quantize_w(3)
+        quantize_pass(3, 1)
         picked2 = fetch(2, 2)
         finish_h(3)
         picked3 = fetch(3, 3)
@@ -311,8 +313,8 @@ def tile_picked_zcbow_soft_p_kernel(
         window_term(2, 1)
         weigh(2, 2, picked2)
         last = TILES - 1
-        round_z(0, 0, last, "w_codes3")
-        round_z(1, 0, last, "w_scale3")
+        round_z(0, 0, last, "w_codes3_1")
+        round_z(1, 0, last, "w_scale3_1")
         for d in range(WHOLE_TERMS):
             window_term(last, d)
         for b in range(HALVES):

@@ -25,8 +25,8 @@ GROUP = 16
 PASSES = K // (P * PACK)
 TILES = H // P
 HALVES = V // P
-V_SCALE_AT, V_SCALE_STEP = 10, 7
-GATE_AT = 24
+V_SCALE_AT, V_SCALE_STEP = 64, 4
+GATE_AT = 40
 WHOLE_TERMS = 0
 
 
@@ -67,36 +67,40 @@ def tile_picked_zcbow_soft_p_kernel(
             nc.vector.tensor_copy(tile[:], table[:].indirect(offsets))
             return tile
 
+        gate_rows = zeroed("gate_rows", [P, P], F32, nc.gpsimd)
         v_scale_table = zeroed("v_scale_table", [P, G], U8, nc.gpsimd)
-        ident = zeroed("ident", [P, P], F32, nc.vector)
-        make_identity(nc, ident[:], nomemset=True)
-        cand_t = load_list("cand_t", cand)
-        x_table = [load_words("x_table0", x_words[0])]
+        x_scale_table = sb("x_scale_table", [P, T], U8)
         offs_t = load_list("offs_t", offs)
-        v_scale_rows = v_scales.shape[1]
+        nc.sync.dma_start(
+            x_scale_table[0:QUADRANT, :].bitcast(I32), x_scales.rearrange("o q c -> q o c").bitcast(I32)
+        )
+        cand_t = load_list("cand_t", cand)
+        nc.vector.memset(x_scale_table[QUADRANT : 2 * QUADRANT, :].bitcast(I32), 0)
+        nc.vector.memset(x_scale_table[2 * QUADRANT : P, :].bitcast(I32), 0)
+        gate_count = D * HALVES
         nc.scalar.dma_start(
+            gate_rows[GATE_AT : GATE_AT + gate_count, :], gate[:, 0, :].rearrange("d (b t) -> d b t", t=P)
+        )
+        v_scale_rows = v_scales.shape[1]
+        nc.gpsimd.dma_start(
             v_scale_table[V_SCALE_AT : V_SCALE_AT + V_SCALE_STEP * v_scale_rows : V_SCALE_STEP, :].bitcast(I32),
             v_scales[0].bitcast(I32),
         )
-        x_scale_table = zeroed("x_scale_table", [P, T], U8, nc.vector)
-        for q, queue in enumerate((nc.scalar, nc.scalar, nc.gpsimd, nc.gpsimd)):
-            queue.dma_start(
-                x_scale_table[QUADRANT * q : QUADRANT * q + ROWS * PASSES, :].bitcast(I32),
-                x_scales[:, ROWS * q : ROWS * (q + 1), :].bitcast(I32),
-            )
-        gate_rows = zeroed("gate_rows", [P, P], F32, nc.vector)
-        v_scale = zeroed("v_scale", [P, R], U8, nc.vector)
-
-        gate_count = D * HALVES
-        nc.sync.dma_start(
-            gate_rows[GATE_AT : GATE_AT + gate_count, :], gate[:, 0, :].rearrange("d (b t) -> d b t", t=P)
-        )
+        ident = zeroed("ident", [P, P], F32, nc.vector)
+        make_identity(nc, ident[:], nomemset=True)
+        x_scale = zeroed("x_scale", [P, PASSES, S], U8, nc.vector)
+        pos_t = [load_list("pos_t0", pos1)]
+        x_table = [load_words("x_table0", x_words[0])]
         w_raw = {(0, o): load_w(0, o) for o in range(PASSES)}
+        pos_t.extend(load_list(f"pos_t{d + 1}", src) for d, src in enumerate((pos2, pos3, pos4)))
         x_table.append(load_words("x_table1", x_words[1]))
-        for o in range(PASSES):
-            w_raw[1, o] = load_w(1, o)
-        pos_t = [load_list(f"pos_t{d}", src) for d, src in enumerate((pos1, pos2, pos3, pos4))]
-        for a in range(2, TILES):
+        x_scale_picked = gather("x_scale_picked", x_scale_table, offs_t[:], U8)
+        for q in range(P // QUADRANT):
+            nc.sync.dma_start(
+                x_scale[QUADRANT * q : QUADRANT * q + ROWS, :, :].bitcast(I32),
+                x_scale_picked[ROWS * PASSES * q : ROWS * PASSES * (q + 1), :].bitcast(I32),
+            )
+        for a in range(1, TILES):
             for o in range(PASSES):
                 w_raw[a, o] = load_w(a, o)
         v_table = load_words("v_table", v_words[0])
@@ -154,26 +158,19 @@ def tile_picked_zcbow_soft_p_kernel(
                 lhsT=(by_pass[a, o][0][:] if a % 2 else w_codes[a][:, o, :]).bitcast(FP8X4),
                 lhsT_scale=by_pass[a, o][1][:] if a % 2 else w_scale[a][:, o, :],
                 rhs=x_codes[o][:, c0:c1].bitcast(FP8X4),
-                rhs_scale=x_scale[ROWS * o : P, c0:c1],
+                rhs_scale=x_scale[:, o, c0:c1],
                 start=(o == 0),
                 stop=(o == PASSES - 1),
             )
 
-        v_scale_picked = gather("v_scale_picked", v_scale_table, cand_t[:], U8)
-        for q in range(P // QUADRANT):
-            first = V_SCALE_AT + V_SCALE_STEP * ROWS * q
-            nc.sync.dma_start(
-                v_scale[QUADRANT * q : QUADRANT * q + ROWS, :].bitcast(I32),
-                v_scale_picked[first : first + V_SCALE_STEP * ROWS : V_SCALE_STEP, :].bitcast(I32),
-            )
         x_codes = [gather("x_codes0", x_table[0], offs_t[:], U32)]
+        v_scale_picked = gather("v_scale_picked", v_scale_table, cand_t[:], U8, "x_table0")
         cast_w(0)
         gate_all = sb("gate_all", [P, D, V], F32, "w_raw0_1")
         for pair, spread in enumerate(spreads):
             nc.scalar.copy(gate_all[:, 2 * pair : 2 * pair + 2, :], spread[:])
-        x_scale = gather("x_scale", x_scale_table, offs_t[:], U8, "x_table0")
         quantize_w(0)
-        x_codes.append(sb("x_codes1", [P, S], U32, "x_scale_table"))
+        x_codes.append(sb("x_codes1", [P, S], U32, "w_bf0"))
         half, quarter = S // 2, S // 4
         groups = [(0, half, "h_bank1"), (half, half + quarter, "y0"), (half + quarter, S, "h_bank0")]
         for c0, c1, bank in groups:
@@ -185,7 +182,8 @@ def tile_picked_zcbow_soft_p_kernel(
             for c0, c1, bank in groups:
                 if g0 <= c0 < g0 + half:
                     project(0, 1, c0, c1, bank)
-        h[0] = sb("h0", [P, S], F32)
+        cast_w(1, "gate_cols")
+        h[0] = sb("h0", [P, S], F32, "w_raw1_0")
         for c0, c1, bank in groups:
             nc.vector.tensor_copy(h[0][:, c0:c1], h_acc[0, c0][:])
 
@@ -285,12 +283,19 @@ def tile_picked_zcbow_soft_p_kernel(
                 nc.scalar.activation(right[:], exps[:, cut:R], ACT.Copy, scale=sums[:, 1:2])
                 nc.scalar.dma_start(rows[:, cut:R], right[:])
 
-        cast_w(1, "gate_cols")
         picked0 = fetch(0, 3)
-        cast_w(2, "w_raw1_0")
+        cast_w(2)
         quantize_pass(1, 0, "w_codes0")
         quantize_pass(1, 1, "w_scale0")
         finish_h(1, "w_raw2_1")
+        v_scale = sb("v_scale", [P, R], U8, "x_table1")
+        nc.vector.memset(v_scale[:].bitcast(I32), 0)
+        for q in range(P // QUADRANT):
+            first = V_SCALE_AT + V_SCALE_STEP * ROWS * q
+            nc.sync.dma_start(
+                v_scale[QUADRANT * q : QUADRANT * q + ROWS, :].bitcast(I32),
+                v_scale_picked[first : first + V_SCALE_STEP * ROWS : V_SCALE_STEP, :].bitcast(I32),
+            )
         picked1 = fetch(1, 3)
         window_term(0, 0)
         window_term(0, 1, "w_raw1_1")

@@ -27,6 +27,8 @@ TILES = H // P
 HALVES = V // P
 V_SCALE_AT, V_SCALE_STEP = 64, 4
 GATE_AT = 40
+SIZE_FLOOR = 2.0**-120
+PIVOT_SHARE = 2.0**-64
 WHOLE_TERMS = 0
 
 
@@ -68,7 +70,9 @@ def tile_picked_zcbow_soft_p_kernel(
             return tile
 
         gate_rows = zeroed("gate_rows", [P, P], F32, nc.gpsimd)
-        v_scale_table = zeroed("v_scale_table", [P, G], U8, nc.gpsimd)
+        ident = zeroed("ident", [P, P], F32, nc.gpsimd)
+        v_scale_table = zeroed("v_scale_table", [P, G], U8, nc.vector)
+        make_identity(nc, ident[:], nomemset=True)
         x_scale_table = sb("x_scale_table", [P, T], U8)
         offs_t = load_list("offs_t", offs)
         nc.sync.dma_start(
@@ -79,15 +83,13 @@ def tile_picked_zcbow_soft_p_kernel(
         nc.vector.memset(x_scale_table[2 * QUADRANT : P, :].bitcast(I32), 0)
         gate_count = D * HALVES
         nc.scalar.dma_start(
-            gate_rows[GATE_AT : GATE_AT + gate_count, :], gate[:, 0, :].rearrange("d (b t) -> d b t", t=P)
+            gate_rows[GATE_AT : GATE_AT + gate_count, :], gate[:, 0, :].rearrange("d (b t) -> b d t", t=P)
         )
         v_scale_rows = v_scales.shape[1]
         nc.gpsimd.dma_start(
             v_scale_table[V_SCALE_AT : V_SCALE_AT + V_SCALE_STEP * v_scale_rows : V_SCALE_STEP, :].bitcast(I32),
             v_scales[0].bitcast(I32),
         )
-        ident = zeroed("ident", [P, P], F32, nc.vector)
-        make_identity(nc, ident[:], nomemset=True)
         x_scale = zeroed("x_scale", [P, PASSES, S], U8, nc.vector)
         pos_t = [load_list("pos_t0", pos1)]
         x_table = [load_words("x_table0", x_words[0])]
@@ -108,19 +110,52 @@ def tile_picked_zcbow_soft_p_kernel(
         gate_turned = psum.tile([P, P], F32, name="gate_turned", tag="h_bank1")
         nc.tensor.transpose(gate_turned[:], gate_rows[:], ident[:])
         gate_cols = sb("gate_cols", [P, gate_count], F32)
-        nc.scalar.copy(gate_cols[:], gate_turned[:, GATE_AT : GATE_AT + gate_count])
+        turned_gate = gate_turned[:, GATE_AT : GATE_AT + gate_count]
+        raw_side = sb("raw_side", [P, HALVES], F32)
+        nc.scalar.activation(raw_side[:], turned_gate[:, D - 1 : gate_count : D], ACT.Sign)
+        nc.scalar.copy(gate_cols[:], turned_gate)
+        last_gate = gate_cols[:, D - 1 : gate_count : D]
+        sizes = sb("sizes", [P, gate_count], F32)
+        margin = sb("margin", [P, HALVES], F32)
+        for b in range(HALVES):
+            frame = slice(D * b, D * (b + 1))
+            nc.scalar.activation(
+                sizes[:, frame],
+                turned_gate[:, frame],
+                ACT.Abs,
+                scale=PIVOT_SHARE,
+                bias=SIZE_FLOOR,
+                accum_out=margin[:, b : b + 1],
+            )
+        side = sb("side", [P, HALVES], F32)
+        nc.scalar.activation(side[:], raw_side[:], ACT.Sign, bias=0.5)
+        pivot = sb("pivot", [P, HALVES], F32)
+        for b in range(HALVES):
+            nc.scalar.activation(
+                pivot[:, b : b + 1],
+                side[:, b : b + 1],
+                ACT.Identity,
+                scale=margin[:, b : b + 1],
+                bias=last_gate[:, b : b + 1],
+            )
+        inverse = sb("inverse", [P, HALVES], F32)
+        nc.vector.reciprocal(inverse[:], pivot[:])
+        ratio = sb("ratio", [P, HALVES, D - 1], F32)
+        nc.vector.tensor_tensor(
+            ratio[:],
+            gate_cols[:].rearrange("p (b d) -> p b d", b=HALVES)[:, :, 0 : D - 1],
+            inverse[:].unsqueeze(2).to_broadcast([P, HALVES, D - 1]),
+            ALU.mult,
+        )
         spreads = []
-        for pair in range(D // 2):
-            spread = psum.tile([P, 2, V], F32, name=f"gate_spread{pair}", tag=f"turned{pair}")
-            for member in range(2):
+        for n, (d0, d1) in enumerate(((0, 2), (2, 3))):
+            spread = psum.tile([P, d1 - d0, V], F32, name=f"gate_spread{n}", tag=f"turned{n}")
+            for d in range(d0, d1):
                 for b in range(HALVES):
-                    col = (2 * pair + member) * HALVES + b
                     nc.tensor.transpose(
-                        spread[:, member, b * P : (b + 1) * P],
-                        gate_cols[:, col : col + 1].to_broadcast([P, P]),
-                        ident[:],
+                        spread[:, d - d0, b * P : (b + 1) * P], ratio[:, b, d : d + 1].to_broadcast([P, P]), ident[:]
                     )
-            spreads.append(spread)
+            spreads.append((d0, d1, spread))
 
         w_bf, w_codes, w_scale, h_acc, h, by_pass = {}, {}, {}, {}, {}, {}
 
@@ -163,14 +198,14 @@ def tile_picked_zcbow_soft_p_kernel(
                 stop=(o == PASSES - 1),
             )
 
-        x_codes = [gather("x_codes0", x_table[0], offs_t[:], U32)]
+        x_codes = [gather("x_codes0", x_table[0], offs_t[:], U32, "inverse")]
         v_scale_picked = gather("v_scale_picked", v_scale_table, cand_t[:], U8, "x_table0")
-        cast_w(0)
-        gate_all = sb("gate_all", [P, D, V], F32, "w_raw0_1")
-        for pair, spread in enumerate(spreads):
-            nc.scalar.copy(gate_all[:, 2 * pair : 2 * pair + 2, :], spread[:])
+        cast_w(0, "side")
+        gate_all = sb("gate_all", [P, D - 1, V], F32, "w_raw0_1")
+        for d0, d1, spread in spreads:
+            nc.scalar.copy(gate_all[:, d0:d1, :], spread[:])
         quantize_w(0)
-        x_codes.append(sb("x_codes1", [P, S], U32, "w_bf0"))
+        x_codes.append(sb("x_codes1", [P, S], U32, "side"))
         half, quarter = S // 2, S // 4
         groups = [(0, half, "h_bank1"), (half, half + quarter, "y0"), (half + quarter, S, "h_bank0")]
         for c0, c1, bank in groups:
@@ -182,7 +217,8 @@ def tile_picked_zcbow_soft_p_kernel(
             for c0, c1, bank in groups:
                 if g0 <= c0 < g0 + half:
                     project(0, 1, c0, c1, bank)
-        cast_w(1, "gate_cols")
+        cast_w(1, "ratio")
+        quantize_pass(1, 0)
         h[0] = sb("h0", [P, S], F32, "w_raw1_0")
         for c0, c1, bank in groups:
             nc.vector.tensor_copy(h[0][:, c0:c1], h_acc[0, c0][:])
@@ -195,6 +231,7 @@ def tile_picked_zcbow_soft_p_kernel(
 
         zt = [psum.tile([P, H], F32, name=f"zt{b}") for b in range(HALVES)]
         z_bf = {}
+        added = {(a, b): 0 for a in range(TILES) for b in range(HALVES)}
 
         def window_term(a, d, tag=None, halves=(0, 1)):
             t0, t1 = halves[0] * P, (halves[-1] + 1) * P
@@ -210,31 +247,32 @@ def tile_picked_zcbow_soft_p_kernel(
                     zt[b][:, a * P : (a + 1) * P],
                     term[:, n * P : (n + 1) * P],
                     ident[:],
-                    start=(d == 0),
-                    stop=(d == D - 1),
+                    start=(added[a, b] == 0),
+                    stop=(added[a, b] == D - 1),
                     is_transpose=True,
                 )
+                added[a, b] = added[a, b] + 1
 
-        def fetch(a, d0):
-            picked = sb(f"picked{a}", [P, D - d0, V], F32)
-            for d in range(d0, D):
-                nc.scalar.activation(picked[:, d - d0, :], h[a][:].indirect(pos_t[d][:]), ACT.Copy)
+        def fetch(a, d, tag=None):
+            picked = sb(f"picked{a}_{d}", [P, V], F32, tag)
+            nc.scalar.activation(picked[:], h[a][:].indirect(pos_t[d][:]), ACT.Copy)
             return picked
 
-        def weigh(a, d0, picked, halves=(0, 1)):
-            t0, t1 = halves[0] * P, (halves[-1] + 1) * P
-            terms = sb(f"weighed{a}_{t0}", [P, D - d0, t1 - t0], F32)
-            nc.vector.tensor_tensor(terms[:], picked[:, :, t0:t1], gate_all[:, d0:D, t0:t1], ALU.mult)
-            for d in range(d0, D):
-                add_term(a, d, terms[:, d - d0, :], halves)
+        def weigh(a, d, picked, tag=None):
+            term = sb(f"weighed{a}_{d}", [P, V], F32, tag)
+            nc.vector.tensor_tensor(term[:], picked[:], gate_all[:, d, :], ALU.mult)
+            add_term(a, d, term[:], (0, 1))
+            return term
 
         def round_z(b, a0, a1, tag=None):
             per_tile = P // PACK
             if a0 == 0:
                 z_bf[b] = sb(f"z_bf{b}", [P, 2, P, 2], BF16, tag)
-            nc.scalar.copy(
+            nc.scalar.activation(
                 z_bf[b][:, :, per_tile * a0 : per_tile * a1, :],
                 zt[b][:, a0 * P : a1 * P].rearrange("t (p u e) -> t u p e", u=2, e=2),
+                ACT.Copy,
+                scale=pivot[:, b : b + 1],
             )
 
         def pack_z(b):
@@ -285,7 +323,6 @@ def tile_picked_zcbow_soft_p_kernel(
 
         picked0 = fetch(0, 3)
         cast_w(2)
-        quantize_pass(1, 0, "w_codes0")
         quantize_pass(1, 1, "w_scale0")
         finish_h(1, "w_raw2_1")
         v_scale = sb("v_scale", [P, R], U8, "x_table1")
@@ -296,36 +333,37 @@ def tile_picked_zcbow_soft_p_kernel(
                 v_scale[QUADRANT * q : QUADRANT * q + ROWS, :].bitcast(I32),
                 v_scale_picked[first : first + V_SCALE_STEP * ROWS : V_SCALE_STEP, :].bitcast(I32),
             )
-        picked1 = fetch(1, 3)
         window_term(0, 0)
         window_term(0, 1, "w_raw1_1")
+        add_term(0, 3, picked0[:], (0, 1))
         quantize_w(2)
-        cast_w(3, "w_scale0", passes=(0,))
-        finish_h(2, "w_raw3_0")
-        cast_w(3, passes=(1,))
-        window_term(0, 2)
-        weigh(0, 3, picked0)
+        window_term(0, 2, "w_raw2_0")
+        cast_w(3, "w_scale0")
+        finish_h(2, "w_raw3_1")
+        picked1 = fetch(1, 3)
         window_term(1, 0)
-        quantize_pass(3, 0)
         window_term(1, 1)
+        quantize_pass(3, 0)
+        window_term(1, 2, "w_raw3_0")
         quantize_pass(3, 1)
+        add_term(1, 3, picked1[:], (0, 1))
         picked2 = fetch(2, 2)
+        plain2 = fetch(2, 3)
         finish_h(3)
         picked3 = fetch(3, 3)
-        window_term(1, 2)
-        weigh(1, 3, picked1)
-        window_term(2, 0, "w_raw3_1")
+        window_term(2, 0)
         window_term(2, 1)
         weigh(2, 2, picked2)
+        add_term(2, 3, plain2[:], (0, 1))
         last = TILES - 1
         round_z(0, 0, last, "w_codes3_1")
         round_z(1, 0, last, "w_scale3_1")
         for d in range(WHOLE_TERMS):
             window_term(last, d)
         for b in range(HALVES):
+            add_term(last, 3, picked3[:, b * P : (b + 1) * P], (b,))
             for d in range(WHOLE_TERMS, D - 1):
                 window_term(last, d, halves=(b,))
-            weigh(last, D - 1, picked3, halves=(b,))
             round_z(b, last, TILES)
         scores = [psum.tile([P, R], F32, name=f"y{b}") for b in range(HALVES)]
         packed0 = pack_z(0)

@@ -220,8 +220,8 @@ def tile_picked_zcbow_soft_p_kernel(
         cast_w(1, "ratio")
         quantize_pass(1, 0)
         h[0] = sb("h0", [P, S], F32, "w_raw1_0")
-        for c0, c1, bank in groups:
-            nc.vector.tensor_copy(h[0][:, c0:c1], h_acc[0, c0][:])
+        for copy, (c0, c1, bank) in zip((nc.vector.tensor_copy, nc.vector.tensor_copy, nc.scalar.copy), groups):
+            copy(h[0][:, c0:c1], h_acc[0, c0][:])
 
         def finish_h(a, tag=None):
             for o in range(PASSES):
@@ -230,7 +230,7 @@ def tile_picked_zcbow_soft_p_kernel(
             nc.scalar.copy(h[a][:], h_acc[a, 0][:])
 
         zt = [psum.tile([P, H], F32, name=f"zt{b}") for b in range(HALVES)]
-        z_bf = {}
+        z_bf, zt_last = {}, {}
         added = {(a, b): 0 for a in range(TILES) for b in range(HALVES)}
 
         def window_term(a, d, tag=None, halves=(0, 1)):
@@ -241,10 +241,17 @@ def tile_picked_zcbow_soft_p_kernel(
             )
             add_term(a, d, term[:], halves)
 
+        def sums_of(a, b):
+            if a < TILES - 1:
+                return zt[b][:, a * P : (a + 1) * P]
+            if b not in zt_last:
+                zt_last[b] = psum.tile([P, P], F32, name=f"zt_last{b}", tag=f"h_bank{b}")
+            return zt_last[b][:]
+
         def add_term(a, d, term, halves):
             for n, b in enumerate(halves):
                 nc.tensor.matmul(
-                    zt[b][:, a * P : (a + 1) * P],
+                    sums_of(a, b),
                     term[:, n * P : (n + 1) * P],
                     ident[:],
                     start=(added[a, b] == 0),
@@ -270,7 +277,7 @@ def tile_picked_zcbow_soft_p_kernel(
                 z_bf[b] = sb(f"z_bf{b}", [P, 2, P, 2], BF16, tag)
             nc.scalar.activation(
                 z_bf[b][:, :, per_tile * a0 : per_tile * a1, :],
-                zt[b][:, a0 * P : a1 * P].rearrange("t (p u e) -> t u p e", u=2, e=2),
+                (zt[b][:, 0 : a1 * P] if a0 == 0 else zt_last[b][:]).rearrange("t (p u e) -> t u p e", u=2, e=2),
                 ACT.Copy,
                 scale=pivot[:, b : b + 1],
             )
@@ -322,9 +329,10 @@ def tile_picked_zcbow_soft_p_kernel(
                 nc.scalar.dma_start(rows[:, cut:R], right[:])
 
         picked0 = fetch(0, 3)
-        cast_w(2)
+        cast_w(2, "w_codes0", passes=(0,))
         quantize_pass(1, 1, "w_scale0")
-        finish_h(1, "w_raw2_1")
+        finish_h(1, "w_raw2_0")
+        cast_w(2, passes=(1,))
         v_scale = sb("v_scale", [P, R], U8, "x_table1")
         nc.vector.memset(v_scale[:].bitcast(I32), 0)
         for q in range(P // QUADRANT):
@@ -336,20 +344,20 @@ def tile_picked_zcbow_soft_p_kernel(
         window_term(0, 0)
         window_term(0, 1, "w_raw1_1")
         add_term(0, 3, picked0[:], (0, 1))
-        quantize_w(2)
-        window_term(0, 2, "w_raw2_0")
-        cast_w(3, "w_scale0")
-        finish_h(2, "w_raw3_1")
-        picked1 = fetch(1, 3)
+        window_term(0, 2)
         window_term(1, 0)
-        window_term(1, 1)
+        quantize_w(2)
+        cast_w(3, "w_scale0")
+        finish_h(2, "w_raw3_0")
+        picked1 = fetch(1, 3)
+        window_term(1, 1, "w_raw2_1")
         quantize_pass(3, 0)
-        window_term(1, 2, "w_raw3_0")
         quantize_pass(3, 1)
+        window_term(1, 2, "w_raw3_1")
         add_term(1, 3, picked1[:], (0, 1))
         picked2 = fetch(2, 2)
-        plain2 = fetch(2, 3)
         finish_h(3)
+        plain2 = fetch(2, 3, "w_codes3_1")
         picked3 = fetch(3, 3)
         window_term(2, 0)
         window_term(2, 1)

@@ -102,9 +102,13 @@ def tile_picked_zcbow_soft_p_kernel(
                 x_scale[QUADRANT * q : QUADRANT * q + ROWS, :, :].bitcast(I32),
                 x_scale_picked[ROWS * PASSES * q : ROWS * PASSES * (q + 1), :].bitcast(I32),
             )
-        for a in range(1, TILES):
+        for a in range(1, TILES - 1):
             for o in range(PASSES):
                 w_raw[a, o] = load_w(a, o)
+        w_last = sb("w_last", [P, PASSES, PACK, P], F32)
+        for o in range(PASSES):
+            rows = w1[o * P * PACK : (o + 1) * P * PACK, (TILES - 1) * P : H]
+            nc.sync.dma_start(w_last[:, o, :, :], rows.rearrange("(p j) c -> p j c", j=PACK))
         v_table = load_words("v_table", v_words[0])
 
         gate_turned = psum.tile([P, P], F32, name="gate_turned", tag="h_bank1")
@@ -159,6 +163,13 @@ def tile_picked_zcbow_soft_p_kernel(
 
         w_bf, w_codes, w_scale, h_acc, h, by_pass = {}, {}, {}, {}, {}, {}
 
+        def cast_both(a, tag):
+            w_bf[a] = sb(f"w_bf{a}", [P, PASSES, P, PACK], BF16, tag)
+            nc.scalar.copy(
+                w_bf[a][:].rearrange("p o (c n) j -> p o c j n", n=4),
+                w_last[:].rearrange("p o j (c n) -> p o c j n", n=4),
+            )
+
         def cast_w(a, tag=None, passes=(0, 1)):
             if passes[0] == 0:
                 w_bf[a] = sb(f"w_bf{a}", [P, PASSES, P, PACK], BF16, tag)
@@ -190,8 +201,8 @@ def tile_picked_zcbow_soft_p_kernel(
                 h_acc[a, c0] = psum.tile([P, c1 - c0], F32, name=f"h_acc{a}_{c0}", tag=bank)
             nc.tensor.matmul_mx(
                 out=h_acc[a, c0][:],
-                lhsT=(by_pass[a, o][0][:] if a % 2 else w_codes[a][:, o, :]).bitcast(FP8X4),
-                lhsT_scale=by_pass[a, o][1][:] if a % 2 else w_scale[a][:, o, :],
+                lhsT=(by_pass[a, o][0][:] if a == 1 else w_codes[a][:, o, :]).bitcast(FP8X4),
+                lhsT_scale=by_pass[a, o][1][:] if a == 1 else w_scale[a][:, o, :],
                 rhs=x_codes[o][:, c0:c1].bitcast(FP8X4),
                 rhs_scale=x_scale[:, o, c0:c1],
                 start=(o == 0),
@@ -316,11 +327,12 @@ def tile_picked_zcbow_soft_p_kernel(
             nc.vector.reciprocal(sums[:, 1:2], sums[:, 0:1])
             rows = out[b * P : (b + 1) * P, :]
             if b < HALVES - 1:
-                res = sb(f"res{b}", [P, R], F32)
-                nc.vector.tensor_scalar(res[:], exps[:], sums[:, 1:2], None, ALU.mult)
-                nc.sync.dma_start(rows, res[:])
+                for c0, c1 in ((0, 192), (192, R)):
+                    res = sb(f"res{b}_{c0}", [P, c1 - c0], F32)
+                    nc.vector.tensor_scalar(res[:], exps[:, c0:c1], sums[:, 1:2], None, ALU.mult)
+                    nc.sync.dma_start(rows[:, c0:c1], res[:])
             else:
-                cut = 320
+                cut = 224
                 left = sb("res_left", [P, cut], F32)
                 right = sb("res_right", [P, R - cut], F32)
                 nc.vector.tensor_scalar(left[:], exps[:, 0:cut], sums[:, 1:2], None, ALU.mult)
@@ -347,25 +359,24 @@ def tile_picked_zcbow_soft_p_kernel(
         window_term(0, 2)
         window_term(1, 0)
         quantize_w(2)
-        cast_w(3, "w_scale0")
-        finish_h(2, "w_raw3_0")
+        cast_both(3, "w_scale0")
+        finish_h(2)
         picked1 = fetch(1, 3)
         window_term(1, 1, "w_raw2_1")
-        quantize_pass(3, 0)
-        quantize_pass(3, 1)
-        window_term(1, 2, "w_raw3_1")
+        quantize_w(3)
+        window_term(1, 2, "w_last")
         add_term(1, 3, picked1[:], (0, 1))
         picked2 = fetch(2, 2)
         finish_h(3)
-        plain2 = fetch(2, 3, "w_codes3_1")
+        plain2 = fetch(2, 3, "w_codes3")
         picked3 = fetch(3, 3)
         window_term(2, 0)
         window_term(2, 1)
         weigh(2, 2, picked2)
         add_term(2, 3, plain2[:], (0, 1))
         last = TILES - 1
-        round_z(0, 0, last, "w_codes3_1")
-        round_z(1, 0, last, "w_scale3_1")
+        round_z(0, 0, last, "w_codes3")
+        round_z(1, 0, last, "w_scale3")
         for d in range(WHOLE_TERMS):
             window_term(last, d)
         for b in range(HALVES):

from contextlib import ExitStack

import concourse.mybir as mybir
from concourse.masks import make_identity

K, T, S, D, V, H, G, R = 1024, 2048, 512, 4, 256, 512, 2048, 512
FLOPS = 2 * K * H * S + 2 * H * V * R

F32 = mybir.dt.float32
BF16 = mybir.dt.bfloat16
I32 = mybir.dt.int32
U32 = mybir.dt.uint32
U16 = mybir.dt.uint16
U8 = mybir.dt.uint8
FP8X4 = mybir.dt.float8_e4m3fn_x4
ACT = mybir.ActivationFunctionType
ALU = mybir.AluOpType
AXIS = mybir.AxisListType

P = 128
PACK = 4
QUADRANT = 32
ROWS = 4
GROUP = 16
PASSES = K // (P * PACK)
TILES = H // P
HALVES = V // P
V_SCALE_AT, V_SCALE_STEP = 64, 4
GATE_AT = 40
SIZE_FLOOR = 2.0**-120
PIVOT_SHARE = 2.0**-64
WHOLE_TERMS = 0


def tile_picked_zcbow_soft_p_kernel(
    tc, x_words, x_scales, w1, gate, v_words, v_scales, offs, pos1, pos2, pos3, pos4, cand, out
):
    nc = tc.nc
    with ExitStack() as ctx:
        keep = ctx.enter_context(tc.tile_pool(name="keep", bufs=1))
        psum = ctx.enter_context(tc.psum_pool(name="psum", bufs=1))

        def sb(name, shape, dtype, tag=None):
            return keep.tile(shape, dtype, name=name, tag=tag or name, align_bytes=64)

        def zeroed(name, shape, dtype, engine):
            tile = sb(name, shape, dtype)
            engine.memset(tile[:].bitcast(I32), 0)
            return tile

        def load_list(name, src):
            tile = keep.tile(list(src.shape), U16, name=name)
            nc.sync.dma_start(tile[:], src)
            return tile

        def load_words(name, src):
            tile = sb(name, [P, T], U32)
            nc.sync.dma_start(tile[:].bitcast(I32), src.rearrange("p n j -> p (n j)").bitcast(I32))
            return tile

        def load_w(a, o):
            tile = sb(f"w_raw{a}_{o}", [P, PACK, P], F32)
            rows = w1[o * P * PACK : (o + 1) * P * PACK, a * P : (a + 1) * P]
            nc.sync.dma_start(tile[:], rows.rearrange("(p j) c -> p j c", j=PACK))
            return tile

        def gather(name, table, offsets, dtype, tag=None):
            tile = sb(name, [P, offsets.shape[1] * GROUP], dtype, tag)
            nc.vector.tensor_copy(tile[:], table[:].indirect(offsets))
            return tile

        gate_rows = zeroed("gate_rows", [P, P], F32, nc.gpsimd)
        ident = zeroed("ident", [P, P], F32, nc.gpsimd)
        v_scale_table = zeroed("v_scale_table", [P, G], U8, nc.vector)
        make_identity(nc, ident[:], nomemset=True)
        x_scale_table = sb("x_scale_table", [P, T], U8)
        offs_t = load_list("offs_t", offs)
        nc.sync.dma_start(
            x_scale_table[0:QUADRANT, :].bitcast(I32), x_scales.rearrange("o q c -> q o c").bitcast(I32)
        )
        cand_t = load_list("cand_t", cand)
        nc.vector.memset(x_scale_table[QUADRANT : 2 * QUADRANT, :].bitcast(I32), 0)
        nc.vector.memset(x_scale_table[2 * QUADRANT : P, :].bitcast(I32), 0)
        gate_count = D * HALVES
        nc.scalar.dma_start(
            gate_rows[GATE_AT : GATE_AT + gate_count, :], gate[:, 0, :].rearrange("d (b t) -> b d t", t=P)
        )
        v_scale_rows = v_scales.shape[1]
        nc.gpsimd.dma_start(
            v_scale_table[V_SCALE_AT : V_SCALE_AT + V_SCALE_STEP * v_scale_rows : V_SCALE_STEP, :].bitcast(I32),
            v_scales[0].bitcast(I32),
        )
        x_scale = zeroed("x_scale", [P, PASSES, S], U8, nc.vector)
        pos_t = [load_list("pos_t0", pos1)]
        x_table = [load_words("x_table0", x_words[0])]
        w_raw = {(0, o): load_w(0, o) for o in range(PASSES)}
        pos_t.extend(load_list(f"pos_t{d + 1}", src) for d, src in enumerate((pos2, pos3, pos4)))
        x_table.append(load_words("x_table1", x_words[1]))
        x_scale_picked = gather("x_scale_picked", x_scale_table, offs_t[:], U8)
        for q in range(P // QUADRANT):
            nc.sync.dma_start(
                x_scale[QUADRANT * q : QUADRANT * q + ROWS, :, :].bitcast(I32),
                x_scale_picked[ROWS * PASSES * q : ROWS * PASSES * (q + 1), :].bitcast(I32),
            )
        for a in range(1, TILES - 1):
            for o in range(PASSES):
                w_raw[a, o] = load_w(a, o)
        w_last = sb("w_last", [P, PASSES, PACK, P], F32)
        for o in range(PASSES):
            rows = w1[o * P * PACK : (o + 1) * P * PACK, (TILES - 1) * P : H]
            nc.sync.dma_start(w_last[:, o, :, :], rows.rearrange("(p j) c -> p j c", j=PACK))
        v_table = load_words("v_table", v_words[0])

        gate_turned = psum.tile([P, P], F32, name="gate_turned", tag="h_bank1")
        nc.tensor.transpose(gate_turned[:], gate_rows[:], ident[:])
        gate_cols = sb("gate_cols", [P, gate_count], F32)
        turned_gate = gate_turned[:, GATE_AT : GATE_AT + gate_count]
        raw_side = sb("raw_side", [P, HALVES], F32)
        nc.scalar.activation(raw_side[:], turned_gate[:, D - 1 : gate_count : D], ACT.Sign)
        nc.scalar.copy(gate_cols[:], turned_gate)
        last_gate = gate_cols[:, D - 1 : gate_count : D]
        sizes = sb("sizes", [P, gate_count], F32)
        margin = sb("margin", [P, HALVES], F32)
        for b in range(HALVES):
            frame = slice(D * b, D * (b + 1))
            nc.scalar.activation(
                sizes[:, frame],
                turned_gate[:, frame],
                ACT.Abs,
                scale=PIVOT_SHARE,
                bias=SIZE_FLOOR,
                accum_out=margin[:, b : b + 1],
            )
        side = sb("side", [P, HALVES], F32)
        nc.scalar.activation(side[:], raw_side[:], ACT.Sign, bias=0.5)
        pivot = sb("pivot", [P, HALVES], F32)
        for b in range(HALVES):
            nc.scalar.activation(
                pivot[:, b : b + 1],
                side[:, b : b + 1],
                ACT.Identity,
                scale=margin[:, b : b + 1],
                bias=last_gate[:, b : b + 1],
            )
        inverse = sb("inverse", [P, HALVES], F32)
        nc.vector.reciprocal(inverse[:], pivot[:])
        ratio = sb("ratio", [P, HALVES, D - 1], F32)
        nc.vector.tensor_tensor(
            ratio[:],
            gate_cols[:].rearrange("p (b d) -> p b d", b=HALVES)[:, :, 0 : D - 1],
            inverse[:].unsqueeze(2).to_broadcast([P, HALVES, D - 1]),
            ALU.mult,
        )
        spreads = []
        for n, (d0, d1) in enumerate(((0, 2), (2, 3))):
            spread = psum.tile([P, d1 - d0, V], F32, name=f"gate_spread{n}", tag=f"turned{n}")
            for d in range(d0, d1):
                for b in range(HALVES):
                    nc.tensor.transpose(
                        spread[:, d - d0, b * P : (b + 1) * P], ratio[:, b, d : d + 1].to_broadcast([P, P]), ident[:]
                    )
            spreads.append((d0, d1, spread))

        w_bf, w_codes, w_scale, h_acc, h, by_pass = {}, {}, {}, {}, {}, {}

        def cast_both(a, tag):
            w_bf[a] = sb(f"w_bf{a}", [P, PASSES, P, PACK], BF16, tag)
            nc.scalar.copy(
                w_bf[a][:].rearrange("p o (c n) j -> p o c j n", n=4),
                w_last[:].rearrange("p o j (c n) -> p o c j n", n=4),
            )

        def cast_w(a, tag=None, passes=(0, 1)):
            if passes[0] == 0:
                w_bf[a] = sb(f"w_bf{a}", [P, PASSES, P, PACK], BF16, tag)
            for o in passes:
                nc.scalar.copy(
                    w_bf[a][:, o, :, :].rearrange("p (c n) j -> p c j n", n=4),
                    w_raw[a, o][:].rearrange("p j (c n) -> p c j n", n=4),
                )

        def quantize_w(a, tag=None):
            w_codes[a] = sb(f"w_codes{a}", [P, PASSES, P], U32, tag)
            w_scale[a] = sb(f"w_scale{a}", [P, PASSES, P], U8)
            nc.vector.quantize_mx(
                out=w_codes[a][:].rearrange("p o c -> p (o c)").bitcast(FP8X4),
                scales=w_scale[a][:].rearrange("p o c -> p (o c)"),
                in_=w_bf[a][:].rearrange("p o c j -> p (o c j)"),
            )

        def quantize_pass(a, o, tag=None):
            codes = sb(f"w_codes{a}_{o}", [P, P], U32, tag)
            scale = sb(f"w_scale{a}_{o}", [P, P], U8)
            nc.vector.quantize_mx(
                out=codes[:].bitcast(FP8X4), scales=scale[:], in_=w_bf[a][:, o, :, :].rearrange("p c j -> p (c j)")
            )
            by_pass[a, o] = codes, scale

        def project(a, o, c0, c1, bank):
            if o == 0:
                h_acc[a, c0] = psum.tile([P, c1 - c0], F32, name=f"h_acc{a}_{c0}", tag=bank)
            nc.tensor.matmul_mx(
                out=h_acc[a, c0][:],
                lhsT=(by_pass[a, o][0][:] if a == 1 else w_codes[a][:, o, :]).bitcast(FP8X4),
                lhsT_scale=by_pass[a, o][1][:] if a == 1 else w_scale[a][:, o, :],
                rhs=x_codes[o][:, c0:c1].bitcast(FP8X4),
                rhs_scale=x_scale[:, o, c0:c1],
                start=(o == 0),
                stop=(o == PASSES - 1),
            )

        x_codes = [gather("x_codes0", x_table[0], offs_t[:], U32, "inverse")]
        v_scale_picked = gather("v_scale_picked", v_scale_table, cand_t[:], U8, "x_table0")
        cast_w(0, "side")
        gate_all = sb("gate_all", [P, D - 1, V], F32, "w_raw0_1")
        for d0, d1, spread in spreads:
            nc.scalar.copy(gate_all[:, d0:d1, :], spread[:])
        quantize_w(0)
        x_codes.append(sb("x_codes1", [P, S], U32, "side"))
        half, quarter = S // 2, S // 4
        groups = [(0, half, "h_bank1"), (half, half + quarter, "y0"), (half + quarter, S, "h_bank0")]
        for c0, c1, bank in groups:
            project(0, 0, c0, c1, bank)
        for g0 in (0, half):
            nc.vector.tensor_copy(
                x_codes[1][:, g0 : g0 + half], x_table[1][:].indirect(offs_t[:, g0 // GROUP : (g0 + half) // GROUP])
            )
            for c0, c1, bank in groups:
                if g0 <= c0 < g0 + half:
                    project(0, 1, c0, c1, bank)
        cast_w(1, "ratio")
        quantize_pass(1, 0)
        h[0] = sb("h0", [P, S], F32, "w_raw1_0")
        for copy, (c0, c1, bank) in zip((nc.vector.tensor_copy, nc.vector.tensor_copy, nc.scalar.copy), groups):
            copy(h[0][:, c0:c1], h_acc[0, c0][:])

        def finish_h(a, tag=None):
            for o in range(PASSES):
                project(a, o, 0, S, f"h_bank{a % 2}")
            h[a] = sb(f"h{a}", [P, S], F32, tag)
            nc.scalar.copy(h[a][:], h_acc[a, 0][:])

        zt = [psum.tile([P, H], F32, name=f"zt{b}") for b in range(HALVES)]
        z_bf, zt_last = {}, {}
        added = {(a, b): 0 for a in range(TILES) for b in range(HALVES)}

        def window_term(a, d, tag=None, halves=(0, 1)):
            t0, t1 = halves[0] * P, (halves[-1] + 1) * P
            term = sb(f"term{a}_{d}_{t0}", [P, t1 - t0], F32, tag)
            nc.vector.tensor_tensor(
                term[:], h[a][:].indirect(pos_t[d][:, t0 // GROUP : t1 // GROUP]), gate_all[:, d, t0:t1], ALU.mult
            )
            add_term(a, d, term[:], halves)

        def sums_of(a, b):
            if a < TILES - 1:
                return zt[b][:, a * P : (a + 1) * P]
            if b not in zt_last:
                zt_last[b] = psum.tile([P, P], F32, name=f"zt_last{b}", tag=f"h_bank{b}")
            return zt_last[b][:]

        def add_term(a, d, term, halves):
            for n, b in enumerate(halves):
                nc.tensor.matmul(
                    sums_of(a, b),
                    term[:, n * P : (n + 1) * P],
                    ident[:],
                    start=(added[a, b] == 0),
                    stop=(added[a, b] == D - 1),
                    is_transpose=True,
                )
                added[a, b] = added[a, b] + 1

        def fetch(a, d, tag=None):
            picked = sb(f"picked{a}_{d}", [P, V], F32, tag)
            nc.scalar.activation(picked[:], h[a][:].indirect(pos_t[d][:]), ACT.Copy)
            return picked

        def weigh(a, d, picked, tag=None):
            term = sb(f"weighed{a}_{d}", [P, V], F32, tag)
            nc.vector.tensor_tensor(term[:], picked[:], gate_all[:, d, :], ALU.mult)
            add_term(a, d, term[:], (0, 1))
            return term

        def round_z(b, a0, a1, tag=None):
            per_tile = P // PACK
            if a0 == 0:
                z_bf[b] = sb(f"z_bf{b}", [P, 2, P, 2], BF16, tag)
            nc.scalar.activation(
                z_bf[b][:, :, per_tile * a0 : per_tile * a1, :],
                (zt[b][:, 0 : a1 * P] if a0 == 0 else zt_last[b][:]).rearrange("t (p u e) -> t u p e", u=2, e=2),
                ACT.Copy,
                scale=pivot[:, b : b + 1],
            )

        def pack_z(b):
            words = z_bf[b][:].rearrange("t u p e -> t (u p e)").bitcast(F32)
            turned = psum.tile([P, 2, P], F32, name=f"turned{b}")
            for u in range(2):
                nc.tensor.transpose(turned[:, u, :], words[:, u * P : (u + 1) * P], ident[:])
            z_in = sb(f"z_in{b}", [P, P * PACK], BF16)
            nc.scalar.copy(
                z_in[:].bitcast(F32).rearrange("p (t u) -> p t u", u=2), turned[:].rearrange("p u t -> p t u")
            )
            z_codes = sb(f"z_codes{b}", [P, P], U32)
            z_scale = sb(f"z_scale{b}", [P, P], U8)
            nc.vector.quantize_mx(out=z_codes[:].bitcast(FP8X4), scales=z_scale[:], in_=z_in[:])
            return z_codes, z_scale

        def score(y, z_codes, z_scale, c0, c1):
            nc.tensor.matmul_mx(
                out=y[:, c0:c1],
                lhsT=z_codes[:].bitcast(FP8X4),
                lhsT_scale=z_scale[:],
                rhs=v_codes[:, c0:c1].bitcast(FP8X4),
                rhs_scale=v_scale[:, c0:c1],
                start=True,
                stop=True,
            )

        def softmax(b, y):
            sums = sb(f"sums{b}", [P, 4], F32)
            neg_max = sb(f"neg_max{b}", [P, 1], F32)
            nc.vector.tensor_reduce(neg_max[:], y[:], AXIS.X, ALU.max, negate=True)
            exps = sb(f"exps{b}", [P, R], F32)
            nc.scalar.activation(exps[:], y[:], ACT.Exp, bias=neg_max[:], accum_out=sums[:, 0:1])
            nc.vector.reciprocal(sums[:, 1:2], sums[:, 0:1])
            rows = out[b * P : (b + 1) * P, :]
            if b < HALVES - 1:
                for c0, c1 in ((0, 192), (192, R)):
                    res = sb(f"res{b}_{c0}", [P, c1 - c0], F32)
                    nc.vector.tensor_scalar(res[:], exps[:, c0:c1], sums[:, 1:2], None, ALU.mult)
                    nc.sync.dma_start(rows[:, c0:c1], res[:])
            else:
                cut = 224
                left = sb("res_left", [P, cut], F32)
                right = sb("res_right", [P, R - cut], F32)
                nc.vector.tensor_scalar(left[:], exps[:, 0:cut], sums[:, 1:2], None, ALU.mult)
                nc.sync.dma_start(rows[:, 0:cut], left[:])
                nc.scalar.activation(right[:], exps[:, cut:R], ACT.Copy, scale=sums[:, 1:2])
                nc.scalar.dma_start(rows[:, cut:R], right[:])

        picked0 = fetch(0, 3)
        cast_w(2, "w_codes0", passes=(0,))
        quantize_pass(1, 1, "w_scale0")
        finish_h(1, "w_raw2_0")
        cast_w(2, passes=(1,))
        v_scale = sb("v_scale", [P, R], U8, "x_table1")
        nc.vector.memset(v_scale[:].bitcast(I32), 0)
        for q in range(P // QUADRANT):
            first = V_SCALE_AT + V_SCALE_STEP * ROWS * q
            nc.sync.dma_start(
                v_scale[QUADRANT * q : QUADRANT * q + ROWS, :].bitcast(I32),
                v_scale_picked[first : first + V_SCALE_STEP * ROWS : V_SCALE_STEP, :].bitcast(I32),
            )
        window_term(0, 0)
        window_term(0, 1, "w_raw1_1")
        add_term(0, 3, picked0[:], (0, 1))
        window_term(0, 2)
        window_term(1, 0)
        quantize_w(2)
        cast_both(3, "w_scale0")
        finish_h(2)
        picked1 = fetch(1, 3)
        window_term(1, 1, "w_raw2_1")
        quantize_w(3)
        window_term(1, 2, "w_last")
        add_term(1, 3, picked1[:], (0, 1))
        picked2 = fetch(2, 2)
        finish_h(3)
        plain2 = fetch(2, 3, "w_codes3")
        picked3 = fetch(3, 3)
        window_term(2, 0)
        window_term(2, 1)
        weigh(2, 2, picked2)
        add_term(2, 3, plain2[:], (0, 1))
        last = TILES - 1
        round_z(0, 0, last, "w_codes3")
        round_z(1, 0, last, "w_scale3")
        for d in range(WHOLE_TERMS):
            window_term(last, d)
        for b in range(HALVES):
            add_term(last, 3, picked3[:, b * P : (b + 1) * P], (b,))
            for d in range(WHOLE_TERMS, D - 1):
                window_term(last, d, halves=(b,))
            round_z(b, last, TILES)
        scores = [psum.tile([P, R], F32, name=f"y{b}") for b in range(HALVES)]
        packed0 = pack_z(0)
        v_codes = sb("v_codes", [P, R], U32, f"term{last}_0_0")
        for c0 in (0, R // 2):
            c1 = c0 + R // 2
            nc.vector.tensor_copy(v_codes[:, c0:c1], v_table[:].indirect(cand_t[:, c0 // GROUP : c1 // GROUP]))
            score(scores[0], *packed0, c0, c1)
        score(scores[1], *pack_z(1), 0, R)
        for b in range(HALVES):
            softmax(b, scores[b])
